import numpy as np, ml_dtypes
CORES = [35,38,43,46]
N = 4
BF = ml_dtypes.bfloat16
def gentries(a):
    return np.ascontiguousarray(a.reshape(8, 16, -1).transpose(0, 2, 1)).reshape(8, -1)
def gtable(e):
    e = np.asarray(e); return np.ascontiguousarray(e.reshape(8, -1, 16).transpose(0, 2, 1)).reshape(128, -1).astype(np.int32)
PL, D, P, T, H, S, Q4 = 4096, 1024, 256, 4, 2, 16, 1024
def entry(rng, *shape):
    return np.where(rng.random(shape) < 0.5, rng.integers(0, PL, shape), PL + rng.integers(0, D, shape))
def parts(rng):
    x = rng.integers(0, 64, (N, 8, 16, PL)); a = entry(rng, N, 8, 16, D); b = entry(rng, N, 8, 16, D); z = rng.integers(0, 64, (N, 8, 16, P))
    v = rng.integers(0, D, (N, 8, P)); p = rng.integers(0, D, (N, 8, P)); w = rng.integers(0, 256, (N, 8, 16)); h = rng.integers(100, 401, (N, 8, 16))
    return x, a, b, z, v, p, w, h
def pack(x, a, b, z, v, p, w, h):
    return {"xl": np.reshape(x, (N, 128, PL)).astype(np.float32).astype(BF), "vdir": np.reshape(a, (N, 128, D)).astype(np.int32), "pdir": np.reshape(b, (N, 128, D)).astype(np.int32),
            "z": np.reshape(z, (N, 128, P)).astype(np.float32).astype(BF), "vn": np.stack([gtable(e) for e in v]), "pn": np.stack([gtable(e) for e in p]),
            "wt": np.reshape(w, (N, 128, 1)).astype(np.int32), "th": np.reshape(h, (N, 128, 1)).astype(np.int32)}
def setup_inputs(rng):
    return pack(*parts(rng))
def setup_inputs_spread(rng):
    x, a, b, z, v, p, w, h = parts(rng)
    x = (np.exp2(6 * rng.random((N, 8, 1, PL))) * rng.random((N, 8, 16, PL))).astype(np.int64); z = (np.exp2(6 * rng.random((N, 8, 1, P))) * rng.random((N, 8, 16, P))).astype(np.int64)
    x = np.minimum(x, 63); z = np.minimum(z, 63)
    def uneven(n, *shape):
        r = rng.random(shape) ** 3
        return np.minimum((n * np.where(rng.random(shape) < 0.5, r, 1 - r)).astype(np.int64), n - 1)
    a = uneven(PL + D, N, 8, 16, D); b = uneven(PL + D, N, 8, 16, D); v = uneven(D, N, 8, P); p = uneven(D, N, 8, P)
    w = np.minimum((np.exp2(8 * rng.random((N, 8, 16))) * rng.random((N, 8, 16))).astype(np.int64), 255)
    h = np.minimum(np.exp2(10 * rng.random((N, 8, 16))).astype(np.int64) - 1, 1008); h[:, :, 3] = 1008; w[:, :, 3] = 255
    return pack(x, a, b, z, v, p, w, h)
def tips(rng, shape, hi, inner):
    e = hi * rng.integers(0, 2, shape); o = np.where(rng.random(shape) < 0.5, rng.choice(np.array(inner), shape), rng.integers(0, hi + 1, shape))
    return np.where(rng.random(shape) < 0.8, e, o)
def setup_inputs_ends(rng):
    m = rng.integers(0, 3, (N, 8, 1, PL)); x = 63 * np.where(m == 2, rng.integers(0, 2, (N, 8, 16, PL)), m)
    m = rng.integers(0, 3, (N, 8, 1, P)); z = 63 * np.where(m == 2, rng.integers(0, 2, (N, 8, 16, P)), m)
    top = PL + D - 1; w = 255 * rng.integers(0, 2, (N, 8, 16)); h = 1008 * rng.integers(0, 2, (N, 8, 16))
    a = tips(rng, (N, 8, 16, D), top, [PL - 1, PL, 1]); b = tips(rng, (N, 8, 16, D), top, [PL - 1, PL, 1])
    v = tips(rng, (N, 8, P), D - 1, [1, D - 2]); p = tips(rng, (N, 8, P), D - 1, [1, D - 2])
    for g in (0, 7):
        w[:, g] = 255; h[:, g, 0] = 0; h[:, g, 1] = 1008; h[:, g, 14] = 0; h[:, g, 15] = 1008
        for c in (0, D - 1):
            x[:, g, :, c] = 0; a[:, g, :, c] = top * rng.integers(0, 2, (N, 16)); b[:, g, :, c] = top * rng.integers(0, 2, (N, 16))
        for c in (Q4 - 2, 2 * Q4 - 2, 3 * Q4 - 2, PL - 2, PL - 1): x[:, g, :, c] = 63
        for i in (0, 1, P - 1): z[:, g, :, i] = 63
        for i in (2, P - 2): z[:, g, :, i] = 0
        for i, c in ((0, D - 1), (1, 0), (2, D - 1), (P - 2, 0), (P - 1, D - 1)): v[:, g, i] = c; p[:, g, i] = c
    return pack(x, a, b, z, v, p, w, h)
def setup_inputs_corners(rng):
    x, a, b, z, v, p, w, h = parts(rng); own = np.arange(D)[None, :]
    h = np.where(rng.random(h.shape) < 0.6, rng.choice(np.array([0, 1, 1007, 1008]), h.shape), h); w = np.where(rng.random(w.shape) < 0.5, rng.choice(np.array([0, 1, 255]), w.shape), w)
    for q in range(N):
        o = rng.permutation(8)
        for g in range(8):
            c = int(o[g])
            if c == 0:
                a[q, g] = rng.integers(0, PL, (16, D)); b[q, g] = rng.integers(0, PL, (16, D))
                k = rng.choice(np.array([0, 15]), P); e = a[q, g][k, v[q, g]]; m = np.arange(P) % 3 == 0
                z[q, g] = np.where(m[None, :], x[q, g][:, e], z[q, g])
            elif c == 1: a[q, g] = PL + rng.integers(0, D, (16, D)); b[q, g] = PL + rng.integers(0, D, (16, D))
            elif c == 2: a[q, g] = PL + rng.integers(0, D, (16, D)); b[q, g] = rng.integers(0, PL, (16, D))
            elif c == 3:
                a[q, g] = np.where(own % 2 == 0, PL + rng.integers(0, D, (16, D)), rng.integers(0, PL, (16, D)))
                b[q, g] = PL + 2 * rng.integers(0, D // 2, (16, D)) + 1; v[q, g] = 2 * rng.integers(0, D // 2, P)
            elif c == 4:
                a[q, g] = PL + own; b[q, g] = PL + own; b[q, g, 8:] = PL + (own + 1) % D
            elif c == 5:
                a[q, g] = rng.choice(np.array([0, PL - 1, PL, PL + D - 1]), (16, D)); b[q, g] = rng.choice(np.array([0, PL - 1, PL, PL + D - 1]), (16, D)); w[q, g] = 0
            elif c == 6:
                a[q, g] = PL + (D - 1) * rng.integers(0, 2, (16, D)); w[q, g] = 255
            else:
                p[q, g] = v[q, g]; v[q, g, 0] = 0; v[q, g, P - 1] = D - 1; p[q, g, 0] = D - 1; p[q, g, P - 1] = 0
    return pack(x, a, b, z, v, p, w, h)
def setup_inputs_crowd(rng):
    x, a, b, z, v, p, w, h = parts(rng)
    for q in range(N):
        for g in range(8):
            c, e = rng.permutation(D)[:P], rng.permutation(D)[:P]; s, t = int(rng.integers(0, D)), int(rng.integers(0, D))
            if g == 0: c[:] = s
            elif g == 1: e[:] = s
            elif g == 2: c[:] = s; e[:] = t
            elif g == 3: c[:] = s; c[P - 1] = (s + 1) % D
            elif g == 4: e[:] = s; e[0] = (s + 1) % D
            elif g == 5: c = rng.choice(np.array([0, D - 1]), P); e = rng.choice(np.array([0, D - 1]), P)
            elif g == 6 and q < N - 1:
                if q % 2 == 0: e[P - 1] = e[0]
                else: c[P - 1] = c[0]
            elif g == 7: c[:] = s; e[:] = t; z[q, g] = z[q, g, :, :1]
            v[q, g] = c; p[q, g] = e
    h[0] = 0; h[N - 1] = 0; h[N - 1, 6, 15] = 1
    x[1] = 56 + (x[1] >> 3); z[1] = 56 + (z[1] >> 3); h[1] = rng.integers(630, 801, (8, 16))
    x[2] = x[2] >> 3; z[2] = 30 * z[2] >> 6; h[2] = rng.integers(480, 761, (8, 16))
    m = 2 * int(rng.integers(10, 20)) + 1; j = rng.permutation(P)[:m]; k = rng.permutation(16)
    z[2, 5][:, j] = rng.integers(45, 52, (16, m)); h[2, 5, k[:5]] = rng.integers(480, 609, 5); h[2, 5, k[5:]] = rng.integers(820, 1009, 11)
    x[N - 1, 6, 0] = 63; z[N - 1, 6, 0] = rng.integers(0, 63, P); n = int(rng.integers(0, PL))
    a[N - 1, 6, 15, v[N - 1, 6, P - 1]] = n; z[N - 1, 6, :, P - 1] = x[N - 1, 6, :, n]
    return pack(x, a, b, z, v, p, w, h)
def setup_inputs_ties(rng):
    x, a, b, z, v, p, w, h = parts(rng)
    for q in range(N):
        few = q in (1, 3)
        for g in range(8):
            if g % 2 == 0:
                y = rng.integers(21 if few else 0, 41, (16, 1)); x[q, g] = y + 3 * rng.integers(0, 6, (1, PL)); z[q, g] = y + 3 * rng.integers(0, 8, (1, P))
                h[q, g] = rng.choice(np.array([0, 1, 48, 49, 96, 97, 144, 145]), 16)
                if few: h[q, g] = np.sum(y) + 48 * rng.integers(1, 6, 16) - rng.permutation(16) // 6
            else:
                x[q, g] = rng.integers(0, 64, (16, 8))[:, rng.integers(0, 8, PL)]
                v[q, g] = rng.permutation(D)[:P]; p[q, g] = rng.permutation(D)[:P]
                if g % 4 == 1: v[q, g, P - 1] = v[q, g, 0]
                else: p[q, g, P - 1] = p[q, g, 0]
                if few: x[q, g] = x[q, g] >> 2; z[q, g] = z[q, g] >> 2; h[q, g] = rng.integers(241, 301, 16)
    m = rng.permutation(3) + 1
    for i, q in ((0, 1), (1, 3)):
        z[q, 7, :, P - 1] = 62; k = rng.permutation(16)[int(m[i]):]; h[q, 7, k] = 1008
    return pack(x, a, b, z, v, p, w, h)
def check_inputs(d):
    bad = []
    for k, hi in (("xl", 63), ("vdir", PL + D - 1), ("pdir", PL + D - 1), ("z", 63), ("vn", D - 1), ("pn", D - 1), ("wt", 255), ("th", 1008)):
        e = np.asarray(d[k]).astype(np.float64)
        if not (np.min(e) >= 0 and np.max(e) <= hi): bad.append("range of " + k)
        elif not np.all(e == np.floor(e)): bad.append("whole numbers in " + k)
    return bad
def reference(xl, vdir, pdir, z, vn, pn, wt, th):
    X = xl.astype(np.float32).astype(np.int64).reshape(N, 8, 16, PL); Z = z.astype(np.float32).astype(np.int64).reshape(N, 8, 16, P)
    VD = vdir.astype(np.int64).reshape(N, 8, 16, D); PD = pdir.astype(np.int64).reshape(N, 8, 16, D)
    w = wt.astype(np.int64).reshape(N, 8, 16, 1); h = th.astype(np.int64).reshape(N, 8, 16, 1)
    v = np.stack([gentries(a) for a in vn]).astype(np.int64); p = np.stack([gentries(a) for a in pn]).astype(np.int64)
    A = np.zeros(N, np.int64); lower = np.tri(P, P, -1, dtype=bool)
    for t in range(T):
        if t > 0: v, p, Z = np.roll(v, 1, axis=0), np.roll(p, 1, axis=0), np.roll(Z, 1, axis=0)
        e = np.take_along_axis(VD, v[:, :, None, :], 3)
        for i in range(H):
            e = np.where(e >= PL, np.take_along_axis(PD if i % 2 == 0 else VD, np.maximum(e - PL, 0), 3), e)
        e = np.where(e >= PL, e - PL, e)
        x = np.take_along_axis(X, e.reshape(N, 8, 1, 16 * P), 3).reshape(N, 8, 16, 16, P)
        d = np.add.reduce(np.abs(x - Z[:, :, :, None, :]), axis=2)
        ks = np.argmin(d, axis=2)[:, :, None, :]
        xs = np.take_along_axis(x, ks[:, :, None], 3)[:, :, :, 0]
        u = np.add.reduce(w * Z, axis=2) & 4095
        n = S * np.arange(P) + (u & (S - 1))
        near = d < h + (A & 255)[:, None, None, None]
        np.put_along_axis(e, ks, n[:, :, None, :], 2)
        np.put_along_axis(X, n[:, :, None, :], (xs + Z) >> 1, 3)
        same = (v[..., :, None] == v[..., None, :]) | (p[..., :, None] == p[..., None, :])
        edits = ~np.any(same & lower, axis=-1)
        tov = np.where(near, e, PL + p[:, :, None, :]); top = np.where(near, PL + v[:, :, None, :], e)
        for q in range(N):
            for g in range(8):
                m = edits[q, g]
                VD[q, g][:, v[q, g][m]] = tov[q, g][:, m]; PD[q, g][:, p[q, g][m]] = top[q, g][:, m]
        A = np.add.reduce((1 - near.astype(np.int64)).reshape(N, -1), axis=1)
        p, v = v, ((u * u >> 5) + 37 * v) & (D - 1)
        Z = np.abs(Z - xs)
    yx = X[..., :Q4] + 64 * X[..., Q4:2 * Q4] + 4096 * X[..., 2 * Q4:3 * Q4] + 262144 * X[..., 3 * Q4:]
    return {"yx": yx.reshape(N, 128, Q4).astype(np.float32), "yvd": VD.reshape(N, 128, D).astype(np.float32), "ypd": PD.reshape(N, 128, D).astype(np.float32),
            "yz": Z.reshape(N, 128, P).astype(np.float32).astype(BF), "yvp": (D * p + v).astype(np.float32)}

@@ -1,0 +1,710 @@
+from concourse.bass import DstId, RemoteDMATransfer
+from concourse.mybir import AluOpType as OP, AxisListType, ActivationFunctionType as AF
+
+NV = 4
+CH = 64
+NCH = 256 // CH
+L2S = (1, 2, 3)
+XV = (0, 0, 32, 32)
+B2, B3 = ("E0", "K1", "K0", "K1"), ("E1", "E0", "E1", "E0")
+CHAIN = {"G": 1, "Ab": 1, "GF0": 1, "GF1": 1, "GF2": 1, "GH0": 3, "GH1": 3, "GH2": 3, "GL0": 2, "GL1": 2, "GL2": 2}
+EARLY = False
+L2G = (1, 2, 3)
+NB = (("K0", "K0"), ("D0", "D1"))
+UFIRST = True
+BZ, BU = 2500.0, 0.0
+PLAN = []
+SEQ = "20 21 30 22 31 23 32 33"
+TAIL = ((0, 128), (128, 192), (192, 256))
+WW = 6664
+f32, bf, f16, i32, u16 = "float32", "bfloat16", "float16", "int32", "uint16"
+
+
+def _sb(n, d):
+    return ("sbuf", [128] + (n if isinstance(n, list) else [n]), d)
+
+
+SCRATCH = {
+    "W": _sb(WW, f32), "X": _sb(4096, bf), "G": _sb(4096, bf), "Ab": _sb(4096, bf),
+    "rv": _sb(1024, i32), "rp": _sb(1024, i32), "vni": _sb(16, i32), "pni": _sb(16, i32),
+    "wti": _sb(1, i32), "thi": _sb(1, i32),
+    "GL0": _sb(1024, f16), "GL1": _sb(1024, f16), "GL2": _sb(1024, f16), "GF0": _sb(1024, f32), "GF1": _sb(1024, f32),
+    "GF2": _sb(1024, f32), "GH0": _sb(1024, f16), "GH1": _sb(1024, f16), "GH2": _sb(1024, f16),
+    "o1": _sb(16, u16), "o2": _sb(256, u16), "o3": _sb(256, u16), "o4": _sb(256, u16),
+    "os": _sb(32, u16), "on": _sb(16, u16), "ox": _sb(16, u16), "oc": _sb(16, u16),
+    "F1": _sb(2048, bf), "F1f": _sb(2048, f32), "F3": _sb(2048, bf), "mk": _sb(16, f32), "of": _sb(2, u16),
+    "Z16": _sb(144, bf), "Zw": _sb(144, bf), "Zk": _sb(144, bf),
+    "Id": _sb(128, bf), "In": _sb(128, bf), "I2": _sb(128, bf), "Ip": _sb(128, bf), "Im": _sb(128, bf),
+    "I3": _sb(128, bf), "Ik": _sb(128, bf), "Ia": _sb(128, bf), "Ib": _sb(128, bf), "Ic": _sb(128, bf), "Iq": _sb(128, bf),
+    "Bk": _sb(128, bf), "Bi": _sb(128, f32), "onef": _sb(128, f32), "oneb": _sb(256, bf), "m128": _sb(256, bf),
+    "F4": _sb(2048, bf), "mk2": _sb(16, f32), "rf": _sb(512, f32), "d0": _sb(256, f32),
+    "Jz": _sb(512, f16), "Jh": _sb(16, f16), "Jd": _sb(32, f32), "ji": _sb(16, i32),
+    "pi": _sb(1, i32), "ci": _sb(4, i32), "cf": _sb(8, f32),
+    "E": _sb(4096, bf), "dsg": _sb(256, bf), "mm": _sb(256, f32),
+    "kU": _sb(256, f32), "sc": _sb(256, f32), "ohU": _sb(256, bf), "oh": _sb(256, bf), "t1": _sb(256, f32),
+    "ee": _sb(256, f32), "sg": _sb(256, bf), "Q": _sb(512, f32), "nr": _sb(256, f32), "acc": _sb(4, f32),
+    "thr": _sb(1, f32), "ai": _sb(2, i32), "xs": _sb(256, bf), "xr": _sb(256, bf),
+    "ui": _sb(64, i32), "uf": _sb(64, f32), "lh": _sb(32, f16), "vnr": _sb(256, f16), "dl": _sb(64, f32),
+    "OV": _sb(1280, f32), "OPD": _sb(1280, f32), "OX": _sb(1024, f32), "OVP": _sb(256, f32),
+}
+for _t in range(NV):
+    SCRATCH["zz%d" % _t] = _sb(256, bf)
+    SCRATCH["zn%d" % _t] = _sb(256, bf)
+    SCRATCH["rw%d" % _t] = _sb(512, f16)
+    SCRATCH["ls%d" % _t] = _sb(64, f32)
+    SCRATCH["lo%d" % _t] = _sb(64, f32)
+    SCRATCH["vr%d" % _t] = _sb(256, f16)
+PS = ["D0", "D1", "E0", "E1", "K0", "K1", "PV", "M"]
+for _n in PS:
+    SCRATCH[_n] = ("psum", [128, 512], f32)
+ENG = "VSPGY"
+NDMA = 24
+SEMAPHORES = ["eV", "eS", "eP", "eG", "sent"] + ["d%d" % i for i in range(NDMA)] + ["a%d" % i for i in range(12)]
+
+COSTS = [(1.04, 0.52, 60.0, 1.56, 3.8, 110.0, 40.0), (1.04, 0.52, 60.0, 1.1, 2.0, 110.0, 40.0), (1.04, 0.52, 60.0, 2.0, 5.5, 110.0, 40.0),
+         (1.04, 0.42, 30.0, 1.56, 3.8, 60.0, 20.0), (1.04, 0.7, 60.0, 1.56, 3.8, 110.0, 40.0), (1.04, 0.52, 60.0, 1.56, 3.8, 250.0, 120.0)]
+ROUNDS, SLACK = 5000, 1500.0
+
+
+def build(g, T, core, topo, C):
+    CY, PCY, FIX, GA, SCA = C[:5]
+    ops = []
+    rank = T.rank_of(core)
+    nxt = T.cores[(rank + 1) % len(T.cores)]
+    rid, pid, _ = topo.addr(nxt)
+    engs = topo.engines(core, nxt)
+    V, S, P = g.vector, g.scalar, g.tensor
+    nd, na = [0], [0]
+
+    def A(name, lo=None, hi=None, step=None):
+        t = T[name]
+        n = 1
+        for s in t.shape[1:]:
+            n *= s
+        if lo is None:
+            return (t[:], name, 0, n, n)
+        if step is None:
+            return (t[:, lo:hi], name, lo, hi, hi - lo)
+        return (t[:, lo:hi:step], name, lo, hi, len(range(lo, hi, step)))
+
+    def V3(name, ap, n):
+        return (ap, name, 0, 1 << 20, n)
+
+    def IND(win, off):
+        return (win[0].indirect(off[0]), win[1], win[2], win[3], 16 * off[4], off)
+
+    def add(eng, fn, outs, ins, dur, kind="c", extra=None):
+        rd, wr = [], []
+        for a in ins:
+            if isinstance(a, tuple):
+                rd.append(a[1:4])
+                if len(a) > 5:
+                    rd.append(a[5][1:4])
+        for a in outs:
+            wr.append(a[1:4])
+            if len(a) > 5:
+                rd.append(a[5][1:4])
+        ops.append({"e": eng, "fn": fn, "r": rd, "w": wr, "d": dur, "k": kind, "x": extra})
+
+    def ap(a):
+        return a[0] if isinstance(a, tuple) else a
+
+    def two(a):
+        return SCRATCH[a[1]][2] in (bf, f16, u16)
+
+    def vd(o, i, rate):
+        if len(o) > 5:
+            return FIX + SCA * CY * o[4]
+        if len(i) > 5:
+            return FIX + GA * CY * i[4]
+        return FIX + CY * max(40, rate * o[4])
+
+    def cp(o, i):
+        add("V", lambda: V.tensor_copy(o[0], i[0]), [o], [i], vd(o, i, 0.5 if two(o) and two(i) else 1))
+
+    def ts(o, i, s1, op0, s2=None, op1=None):
+        if op1 is None:
+            fn = lambda: V.tensor_scalar(o[0], i[0], ap(s1), None, op0)
+        else:
+            fn = lambda: V.tensor_scalar(o[0], i[0], ap(s1), ap(s2), op0, op1)
+        add("V", fn, [o], [i, s1, s2], vd(o, i, 0.5 if two(o) and two(i) else 1))
+
+    def tt(o, a, b, op):
+        add("V", lambda: V.tensor_tensor(o[0], a[0], b[0], op), [o], [a, b], vd(o, a, 1 if (a[1] in PS or b[1] in PS) else 2))
+
+    def ms(o, c):
+        add("V", lambda: V.memset(o[0], c), [o], [], vd(o, o, 0.5 if two(o) else 1))
+
+    def tr(o, i):
+        add("V", lambda: V.transpose(o[0], i[0]), [o], [i], vd(o, i, 0.5 if two(o) else 1))
+
+    def act(o, i, f, bias=0.0, scale=1.0, acc=None):
+        if acc is None:
+            fn = lambda: S.activation(o[0], i[0], f, bias=ap(bias), scale=ap(scale))
+        else:
+            fn = lambda: S.activation(o[0], i[0], f, bias=ap(bias), scale=ap(scale), accum_out=acc[0])
+        add("S", fn, [o] + ([acc] if acc else []), [i, bias, scale], FIX + CY * (GA if len(i) > 5 else 1) * max(40, i[4]))
+
+    def mm(lst):
+        def fn():
+            r = None
+            for o, l, x, st, sp in lst:
+                r = P.matmul(o[0], l[0], x[0], st, sp)
+            return r
+        d = sum(max(64, x[4]) * (4 if SCRATCH[x[1]][2] == f32 else 1) * PCY + 4 for o, l, x, st, sp in lst)
+        add("P", fn, [m[0] for m in lst], [m[1] for m in lst] + [m[2] for m in lst], d + 30)
+
+    def grp(lst):
+        mm([(o, l, x, n == 0, n == len(lst) - 1) for n, (o, l, x) in enumerate(lst)])
+
+    def iota(o, pat, base, cm):
+        if SCRATCH[o[1]][2] == i32:
+            fn = lambda: g.iota(o[0], pat, base, cm)
+        else:
+            fn = lambda: g.iota(o[0], pat, base, cm, allow_small_or_imprecise_dtypes=True)
+        add("G", fn, [o], [], 160 + 2 * CY * o[4])
+
+    def narrow(o, i):
+        add("G", lambda: g.affine_select(o[0], i[0], [[0, o[4]]], OP.is_ge, 0.0, 0, 0), [o], [i], 210 + 2 * CY * o[4])
+
+    def dma(q, o, i, nbytes, slow=False):
+        sem = T.sem["d%d" % nd[0]]
+        nd[0] += 1
+        Q = {"Y": g.sync, "S": g.scalar, "G": g}[q]
+        if slow:
+            fn = lambda: Q.dma_start(ap(o), ap(i), allow_slow_non_contiguous=True).then_inc(sem, 16)
+        else:
+            fn = lambda: Q.dma_start(ap(o), ap(i)).then_inc(sem, 16)
+        add(q, fn, [o] if isinstance(o, tuple) else [], [i], 1000 if q == "G" else 100, "dma", (sem, 16, 1800 + nbytes / 200.0))
+
+    def send(pairs, per):
+        sem = T.sem["a%d" % na[0]]
+        na[0] += 1
+        trs = []
+        for n, (o, i) in enumerate(pairs):
+            m = 0
+            for e in engs[n * per:(n + 1) * per]:
+                m |= 1 << e
+            trs.append(RemoteDMATransfer(dst_ids=[DstId(rid=rid, pnc=pid)], dma_engine_mask=m, remote_sem=sem, src=i[0], dst=o[0]))
+        if len(pairs) == 1:
+            fn = lambda: g.remote_dma(pairs[0][0][0], pairs[0][1][0], sem, T.sem.sent, pid, rid, m)
+        else:
+            fn = lambda: g.remote_dma_fused(trs, local_sem=T.sem.sent)
+        add("G", fn, [p[0] for p in pairs], [p[1] for p in pairs], 800, "rem", (sem, per * len(pairs), 3500))
+
+    ID, ABS, SIGN, RELU = AF.Identity, AF.Abs, AF.Sign, AF.Relu
+    F = lambda n, k: A(n, 128 * k, 128 * k + 128)
+    Z = lambda n, k: A(n, 15 - k, 143 - k)
+    col = lambda k: A("cf", k, k + 1)
+
+    first = [len(ops)]
+    dma("Y", A("rv", 0, 512), T.vdir[:, 0:512], 262144)
+    dma("S", A("rp", 0, 512), T.pdir[:, 0:512], 2 * 262144)
+    dma("Y", A("rv", 512, 1024), T.vdir[:, 512:1024], 3 * 262144)
+    dma("S", A("rp", 512, 1024), T.pdir[:, 512:1024], 4 * 262144)
+    dma("Y", A("vni"), T.vn[:], 4 * 262144)
+    dma("S", A("pni"), T.pn[:], 4 * 262144)
+    dma("Y", A("zz0"), T.z[:], 4 * 262144)
+    dma("Y", A("X"), T.xl[:], 8 * 262144)
+    iota(A("pi"), [[0, 1]], 0, 1)
+    iota(A("W", 0, 512), [[1, 512]], 4095, 0)
+    for n in range(first[0], len(ops)):
+        ops[n]["b"] = 1.0e6 * (20 - n)
+    iota(A("ji"), [[16, 16]], 0, 0)
+    iota(A("Bi"), [[1, 8], [0, 16]], 0, 0)
+    ops[-1]["b"] = 1.0e5
+    iota(A("W", 3072, 4097), [[1, 1025]], 4095 + 3072, 0)
+    dma("G", A("wti"), T.wt[:], 512, True)
+    dma("G", A("thi"), T.th[:], 512, True)
+    ms(A("F1"), 0.0)
+    cp(col(0), A("pi"))
+    ts(A("ci", 0, 1), A("pi"), 15, OP.bitwise_and)
+    ts(A("ci", 1, 2), A("pi"), 4, OP.arith_shift_right)
+    cp(A("cf", 1, 3), A("ci", 0, 2))
+    ts(A("of", 0, 1), col(1), 128.0, OP.mult, col(0), OP.add)
+    ts(col(7), col(2), 16.0, OP.mult, 4095.0 + 15.0, OP.add)
+    ts(A("mk"), A("W", 0, 16), -4095.0, OP.add, col(1), OP.is_equal)
+    cp(IND(A("F1"), A("of", 0, 1)), A("mk"))
+    for n in range(len(ops) - 9, len(ops)):
+        ops[n]["b"] = 1.0e5
+    ts(A("W", 512, 1024), A("W", 0, 512), 512.0, OP.add)
+    ts(A("W", 1024, 2048), A("W", 0, 1024), 1024.0, OP.add)
+    for b in (2048, 2560):
+        act(A("W", b, b + 512), A("W", 0, 512), ID, bias=float(b))
+    if [c for c in L2S if c not in L2G]:
+        for h in range(2):
+            act(A("F1f", 1024 * h, 1024 * h + 1024), A("F1", 1024 * h, 1024 * h + 1024), ID)
+    ts(A("Id"), A("W", 0, 128), -4095.0, OP.add, col(0), OP.is_equal)
+    for n, c in (("In", -1.0), ("I2", 2.0), ("Ip", 8192.0), ("Im", -8192.0), ("I3", 3072.0), ("Ia", 64.0), ("Ib", 4096.0),
+                 ("Ic", 262144.0), ("Iq", 1024.0)):
+        act(A(n), A("Id"), ID, scale=c)
+    act(A("Ik"), A("Id"), ID, scale=col(1))
+    ms(A("oneb"), 1.0)
+    ms(A("onef"), 1.0)
+    ms(A("m128"), -128.0)
+    ts(A("Jz", 0, 256), A("W", 0, 256), -4095.0, OP.add, 16.0, OP.mult)
+    ts(A("Jz", 256, 512), A("oneb"), 0.0, OP.mult)
+    ts(A("oc"), A("ji"), 15.0, OP.add)
+    ts(A("Jd", 0, 16), A("ji"), col(1), OP.add, 1024.0, OP.add)
+    ts(A("Jd", 16, 32), A("ji"), col(1), OP.add, 1023.5, OP.add)
+    ts(A("Jh"), A("ji"), col(1), OP.add, 16.0, OP.mult)
+    ts(A("Jh", 12, 16), A("Jh", 12, 16), -3072.0, OP.add)
+    ts(A("Z16"), A("W", 0, 144), col(7), OP.is_equal, 16.0, OP.mult)
+    ts(A("Zk"), A("W", 0, 144), col(7), OP.is_equal, col(1), OP.mult)
+    cp(col(5), A("wti"))
+    ts(A("Zw"), A("W", 0, 144), col(7), OP.is_equal, col(5), OP.mult)
+    ts(col(6), A("thi"), 16.0, OP.mult, -0.5, OP.add)
+    ts(A("Bk"), A("Bi"), col(2), OP.is_equal)
+    ops[-1]["b"] = 1.0e5
+    ts(A("mk2"), A("W", 0, 16), -4095.0, OP.add, col(1), OP.is_gt)
+    for s in range(16):
+        act(F("F4", s), A("Bk"), ID, scale=A("mk2", s, s + 1))
+    ms(A("d0"), 0.0)
+    ms(A("d0", 0, 256, 16), 1.0e6)
+    for s in range(16):
+        act(F("F3", s), A("Bk"), ID, scale=A("mk", s, s + 1))
+    VDw, PDw = lambda a, b: A("W", 4098 + 2 * a, 4098 + 2 * b - 1, 2), lambda a, b: A("W", 4097 + 2 * a, 4097 + 2 * b - 1, 2)
+    for h in range(2):
+        ts(A("D0"), A("rv", 512 * h, 512 * h + 512), 4096.0, OP.max)
+        tt(VDw(512 * h, 512 * h + 512), A("rv", 512 * h, 512 * h + 512), A("D0"), OP.add)
+        ts(A("D1"), A("rp", 512 * h, 512 * h + 512), 1.0, OP.add, 4096.0, OP.max)
+        tt(PDw(512 * h, 512 * h + 512), A("rp", 512 * h, 512 * h + 512), A("D1"), OP.add)
+    cp(A("ls0", 0, 16), A("vni"))
+    ts(A("ls0", 16, 32), A("pni"), -0.5, OP.add)
+    cp(A("uf", 32, 48), A("pni"))
+
+    def torows(first):
+        grp(first + [(A("M", s, 512, 16), F("F3", s), A("lh")) for s in range(16)])
+
+    def dups(row, lst, out):
+        for c in range(16):
+            n = 256 - 16 * c
+            ts(A("E", 256 * c, 256 * c + n), A(row[0], row[1] + 16 * c, row[1] + 256), A(lst[0], lst[1] + c, lst[1] + c + 1), OP.is_equal)
+        lst = [(A("M", 0, 256), F("F4", 0), A("oneb"))]
+        lst += [(A("M", 16 * c + 16, 256), A("Bk"), A("E", 256 * c + 16, 240 * c + 256)) for c in range(15)]
+        lst += [(A("M", s, 256, 16), F("F4", s), A("E", s, 4096, 256)) for s in range(1, 16)]
+        for k0 in (0, 6, 16):
+            mm([(o, l, x, n == 0, n == 30) for n, (o, l, x) in enumerate(lst)][k0:{0: 6, 6: 16, 16: 31}[k0]])
+        act(A("dsg"), A("M", 0, 256), SIGN)
+        grp([(A("M", 256, 272), F("F1", s), A("dsg", s, 256, 16)) for s in range(16)])
+        for b in (32, 48):
+            act(A(out, b, b + 16), A("M", 256, 272), ID, scale=2048.0, bias=-1.0)
+
+    cp(A("lh", 0, 16), A("vni"))
+    cp(A("lh", 16, 32), A("pni"))
+    mm([(A("M", s, 512, 16), F("F3", s), A("lh"), True, True) for s in range(16)])
+    act(A("rf"), A("M"), ID)
+    narrow(A("rw0"), A("rf"))
+    dups(("rw0", 256), ("uf", 32), "ls0")
+    ngl, ngf, ne = [0], [0], [0]
+
+    for t in range(NV):
+        last = t == NV - 1
+        zz, zn, rw, ls, lo, vr = ["%s%d" % (n, t) for n in ("zz", "zn", "rw", "ls", "lo", "vr")]
+        if t == 0:
+            thr = col(6)
+        else:
+            grp([(A("M", 0, 1), A("onef"), A("acc", c, c + 1)) for c in range(len(TAIL))])
+            ts(A("ai", 0, 1), A("M", 0, 1), -0.5, OP.mult, 16384.0, OP.add)
+            ts(A("ai", 1, 2), A("ai", 0, 1), 255, OP.bitwise_and)
+            ts(A("thr"), A("ai", 1, 2), 16.0, OP.mult, col(6), OP.add)
+            thr = A("thr")
+        ts(A("o1"), A(ls, 0, 16), 2.0, OP.mult, 2.0, OP.add)
+        for a, b in ((0, 128), (128, 256)):
+            ts(A("o2", a, b), IND(A("W", 4096, 6145), A("o1", a // 16, b // 16)), -4095.0, OP.add)
+        if last:
+            for h in range(2):
+                for n, win, bias in (("OV", VDw, -4096.0), ("OPD", PDw, -4095.5)):
+                    act(A(n, 512 * h, 512 * h + 512), win(512 * h, 512 * h + 512), ID, bias=-4096.0)
+                    act(A("K1"), win(512 * h, 512 * h + 512), RELU, bias=bias, scale=0.5)
+                    tt(A(n, 512 * h, 512 * h + 512), A(n, 512 * h, 512 * h + 512), A("K1"), OP.subtract)
+        def edits():
+            if t == 0 or not EARLY:
+                dups((rw, 0), (ls, 0), lo)
+            tt(A("dl", 0, 32), A(lo, 32, 64), A(ls, 32, 64), OP.max)
+            tt(A("dl", 32, 64), A("dl", 0, 32), A("Jd"), OP.min)
+            tt(A("dl", 0, 32), A("dl", 32, 64), A(ls, 0, 32), OP.max)
+            if last:
+                ts(A("os"), A("dl", 0, 32), 0.25, OP.add)
+            else:
+                ts(A("os"), A("dl", 0, 32), 2.0, OP.mult, 2.0, OP.add)
+
+        if not UFIRST:
+            edits()
+        n0 = len(ops)
+        grp([(A("M", 0, 16), Z("Zw", s), A(zz, s, 256, 16)) for s in range(16)])
+        cp(A("ui", 0, 16), A("M", 0, 16))
+        ts(A("ui", 16, 32), A("ui", 0, 16), 4095, OP.bitwise_and)
+        ts(A("ui", 32, 48), A("ui", 0, 16), 15, OP.bitwise_and)
+        tt(A("uf", 0, 16), A("ui", 16, 32), A("ui", 16, 32), OP.mult)
+        act(A("uf", 16, 32), A(ls, 0, 16), ID, scale=1184.0, bias=-1184.0 * 1024)
+        tt(A("ui", 0, 16), A("uf", 0, 16), A("uf", 16, 32), OP.add)
+        ts(A("ui", 48, 64), A("ui", 0, 16), 5, OP.arith_shift_right, 1023, OP.bitwise_and)
+        cp(A("lh"), A("ui", 32, 64))
+        grp([(A("M", 0, 32), A("Id"), A("lh")), (A("M", 0, 16), A("Id"), A("Jh"))])
+        cp(A("on"), A("M", 0, 16))
+        if not last:
+            act(A(lo, 0, 16), A("M", 16, 32), ID)
+        if last:
+            torows([(A("M"), A("Id"), A("Jz")), (A("M", 256, 512), A("Iq"), A(rw, 0, 256))])
+            act(A("nr"), A("M", 0, 256), ID)
+            act(A("OVP"), A("M", 256, 512), ID)
+            dma("Y", T.yvp[:], (T.OVP[0:128:16, :], "OVP", 0, 256, 256), 8192)
+        else:
+            torows([(A("M"), A("Id"), A("Jz"))])
+            act(A("rf", 0, 256), A("M", 256, 512), ID)
+            narrow(A(vr), A("rf", 0, 256))
+            act(A("nr"), A("M", 0, 256), ID, bias=4096.0)
+            act(A(lo, 16, 32), A(ls, 0, 16), ID, bias=-0.5)
+            send([(A("rw%d" % (t + 1), 0, 256), A(vr)), (A("rw%d" % (t + 1), 256, 512), A(rw, 0, 256))], 4)
+        for o in ops[n0:]:
+            o["b"] = BU
+        if UFIRST:
+            edits()
+        if not last:
+            send([(A("ls%d" % (t + 1)), A(lo))], 4)
+
+        def look2(c):
+            a, b = CH * c, CH * c + CH
+            win = IND(A("W", 0, 6145), A("o2", a, b))
+            if c in L2S:
+                gl, fam = "GF%d" % (ngf[0] % 3), "F1f"
+                ngf[0] += 1
+                act(A(gl), win, ID, bias=-6143.0)
+                if c in L2G:
+                    for h in range(2):
+                        narrow(A("GH" + gl[2], 512 * h, 512 * h + 512), A(gl, 512 * h, 512 * h + 512))
+                    gl, fam = "GH" + gl[2], "F1"
+            else:
+                gl, fam = "GL%d" % (ngl[0] % 3), "F1"
+                ngl[0] += 1
+                ts(A(gl), win, -6143.0, OP.add)
+            e = B2[c]
+            st = 4 if fam == "F1f" else 16
+            for k0 in range(0, 16, st):
+                mm([(A(e, 0, CH), F(fam, k), A(gl, k, 16 * CH, 16), k == 0, k == 15) for k in range(k0, k0 + st)])
+            ts(A("o3", a, b), A(e, 0, CH), 2048.0, OP.add)
+
+        def look3(c):
+            a, b = CH * c, CH * c + CH
+            gl = "GL%d" % (ngl[0] % 3)
+            ngl[0] += 1
+            ts(A(gl), IND(A("W", 0, 6145), A("o3", a, b)), -6144.0, OP.add, 0.5, OP.mult)
+            e = B3[c]
+            grp([(A(e, 0, CH), A("I3"), A("oneb", 0, CH))] + [(A(e, 0, CH), F("F1", k), A(gl, k, 16 * CH, 16)) for k in range(16)])
+            ts(A("mm", a, b), A(e, 0, CH), 4096.0, OP.is_lt, 1.0, OP.add)
+            tt(A("PV", a, b), A(e, 0, CH), A("mm", a, b), OP.mult)
+            ts(A("o4", a, b), A("PV", a, b), -4096.0, OP.add)
+
+        def lines(c):
+            a, b = CH * c, CH * c + CH
+            m = a + XV[c]
+            if m > a:
+                cp(A("G", 16 * a, 16 * m), IND(A("X"), A("o4", a, m)))
+            if m < b:
+                act(A("G", 16 * m, 16 * b), IND(A("X"), A("o4", m, b)), ID)
+            for h in range(2):
+                d = "D%d" % h
+                lst = []
+                for kk in range(8):
+                    o = A(d, CH * kk, CH * kk + CH)
+                    lst += [(o, A("Id"), A("G", 16 * a + 8 * h + kk, 16 * b, 16), True, False), (o, A("In"), A(zz, a, b), False, True)]
+                mm(lst)
+                act(A("Ab", 16 * a + 512 * h, 16 * a + 512 * h + 512), A(d), ABS)
+            kb = "K%d" % ([n for n, r in enumerate(TAIL) if r[0] <= a < r[1]][0] % 2)
+            for h in range(2):
+                mm([(A(kb, a, b), A("Ik"), A("oneb", 0, CH), True, False)] * (1 - h) +
+                   [(A(kb, a, b), Z("Z16", k), A("Ab", 16 * a + CH * k, 16 * a + CH * k + CH), False, k == 15) for k in range(8 * h, 8 * h + 8)])
+
+        def tail(n):
+            a, b = TAIL[n]
+            kb, e = "K%d" % (n % 2), "E%d" % (n % 2)
+            if last:
+                ts(A("PV", a, b), A("PV", a, b), -4096.0, OP.add)
+            tt(A("PV", 256 + a, 256 + b), A("nr", a, b), A("PV", a, b), OP.subtract)
+            tr(A("kU", a, b), A(kb, a, b))
+            act(A("sg", a, b), A(kb, a, b), SIGN, bias=thr, scale=-1.0, acc=None if last else A("acc", n, n + 1))
+            o, d0, d1 = A("sc", a, b), A("d0", a, b), A("kU", a, b)
+            add("V", lambda: V.tensor_tensor_scan(o[0], d0[0], d1[0], 0.0, OP.add, OP.min), [o], [d0, d1], FIX + CY * (b - a))
+            tt(A("ohU", a, b), IND(A("sc", a, b), A("oc", 0, (b - a) // 16)), A("kU", a, b), OP.is_equal)
+            tr(A("oh", a, b), A("ohU", a, b))
+            wq = A("Id") if last else A("I2")
+            mm([(A(e, a, b), wq, A(rw, 256 + a, 256 + b), True, False), (A(e, a, b), A("Im"), A("sg", a, b), False, True),
+                (A(e, 256 + a, 256 + b), wq, A(rw, a, b), True, False), (A(e, 256 + a, 256 + b), A("Ip"), A("sg", a, b), False, True)])
+            act(A("Q", a, b), A(e, a, b), ID, bias=-4096.0 if last else 0.0)
+            act(A("Q", 256 + a, 256 + b), A(e, 256 + a, 256 + b), ID, bias=-4096.0 if last else 1.0)
+            tt(A("t1", a, b), A("oh", a, b), A("PV", 256 + a, 256 + b), OP.mult)
+            tt(A("ee", a, b), A("t1", a, b), A("PV", a, b), OP.add)
+            wv, wp = (A("OV"), A("OPD")) if last else (A("W", 4096, WW), A("W", 4096, WW))
+            tt(IND(wv, A("os", a // 16, b // 16)), A("ee", a, b), A("Q", a, b), OP.max)
+            tt(IND(wp, A("os", 16 + a // 16, 16 + b // 16)), A("ee", a, b), A("Q", 256 + a, 256 + b), OP.max)
+
+        def nearest(a, b, bl, bx):
+            ca, cb = a // 16, b // 16
+            grp([(A(bl, ca, cb), A("Id"), A("Jh", ca, cb))] + [(A(bl, ca, cb), Z("Zk", s), A("oh", a + s, b, 16)) for s in range(16)])
+            cp(A("ox", ca, cb), A(bl, ca, cb))
+            act(A("xs", a, b), IND(A("G", 16 * a, 16 * b), A("ox", ca, cb)), ID)
+            mm([(A(bx, a, b), A("Id"), A("xs", a, b), True, False), (A(bx, a, b), A("Id"), A(zz, a, b), False, True),
+                (A(bx, 256 + a, 256 + b), A("Id"), A("xs", a, b), True, False), (A(bx, 256 + a, 256 + b), A("In"), A(zz, a, b), False, True)])
+            if not last:
+                act(A(zn, a, b), A(bx, 256 + a, 256 + b), ABS)
+            act(A("xr", a, b), A(bx, a, b), ID, bias=127.75, scale=0.5)
+            tt(IND(A("X", 16 * a, 16 * b), A("on", ca, cb)), A("xr", a, b), A("m128", a, b), OP.add)
+            if last:
+                act(A(zn, a, b), A(bx, 256 + a, 256 + b), ABS)
+
+        for w in SEQ.split():
+            (look2 if w[0] == "2" else look3)(int(w[1]))
+        for c in range(NCH):
+            lines(c)
+            for n, r in enumerate(TAIL):
+                if r[1] == CH * c + CH:
+                    tail(n)
+        if last:
+            dma("Y", T.yvd[:], A("OV", 0, 1024), 524288)
+            dma("S", T.ypd[:], A("OPD", 0, 1024), 1000000)
+            yx = lambda h, qs: mm([(A("D%d" % h), A(("Id", "Ia", "Ib", "Ic")[q]), A("X", 1024 * q + 512 * h, 1024 * q + 512 * h + 512),
+                                    q == 0, q == 3) for q in qs])
+            nearest(0, 192, "M", "M")
+            yx(0, (0, 1, 2))
+            yx(1, (0, 1, 2))
+            nearest(192, 256, "K1", "K1")
+            dma("Y", T.yz[:], A(zn), 65536)
+            for h in range(2):
+                yx(h, (3,))
+                if h == 0:
+                    act(A("OX", 0, 512), A("D0"), ID)
+                else:
+                    cp(A("OX", 512, 1024), A("D1"))
+                dma("S" if h == 0 else "Y", T.yx[:, 512 * h:512 * h + 512], A("OX", 512 * h, 512 * h + 512), 600000)
+        else:
+            for (a, b), bk in zip(((0, 192), (192, 256)), NB):
+                n0 = len(ops)
+                nearest(a, b, bk[0], bk[1])
+                send([(A("zz%d" % (t + 1), a, b), A(zn, a, b))], 4)
+                for o in ops[n0:n0 + 5] + ops[-1:]:
+                    o["b"] = BZ
+            if EARLY:
+                dups(("rw%d" % (t + 1), 0), ("ls%d" % (t + 1), 0), "lo%d" % (t + 1))
+    return ops
+
+
+def depend(ops):
+    deps = [set() for _ in ops]
+    hist = {}
+    for i, o in enumerate(ops):
+        for lst, wr in ((o["r"], False), (o["w"], True)):
+            for name, lo, hi in lst:
+                for j, l2, h2, w2 in hist.get(name, ()):
+                    if j != i and (((wr or w2) and lo < h2 and l2 < hi) or (name in PS and (ops[j]["e"] != o["e"] or o["e"] == "P"))):
+                        deps[i].add(j)
+        for lst, wr in ((o["r"], False), (o["w"], True)):
+            for name, lo, hi in lst:
+                h = hist.setdefault(name, [])
+                if wr:
+                    h[:] = [x for x in h if not (lo <= x[1] and x[2] <= hi and (name not in PS or ops[x[0]]["e"] == o["e"]))]
+                h.append((i, lo, hi, wr))
+    return deps
+
+
+def key(o):
+    nm = lambda a: (a[0][:2] if a[0][:2] in ("zn", "zz", "lo", "ls", "rw", "vr", "GL", "GF", "GH") else a[0]) + str(a[1])
+    return o["e"] + "".join(nm(a) for a in o["w"][:1] + o["r"][-1:])
+
+
+def replay(ops, order, deps, C):
+    free, fin, end = {e: 0.0 for e in ENG}, [0.0] * len(ops), 0.0
+    for i in order:
+        o = ops[i]
+        e = o["e"]
+        s = free[e]
+        for j in deps[i]:
+            d = ops[j]
+            x = fin[j] + (d["x"][2] if d["k"] != "c" else C[5] if d["e"] != e else 0 if e == "P" else C[6])
+            if x > s:
+                s = x
+        fin[i] = free[e] = s + o["d"]
+        end = max(end, fin[i] + (o["x"][2] if o["k"] != "c" else 0))
+    return end
+
+
+def search(g, T, core, topo):
+    vs = [build(g, T, core, topo, C) for C in COSTS]
+    deps = depend(vs[0])
+    ops, C = vs[0], COSTS[0]
+    n = len(ops)
+    gap = lambda j, i: ops[j]["x"][2] if ops[j]["k"] != "c" else C[5] if ops[j]["e"] != ops[i]["e"] else 0 if ops[j]["e"] == "P" else C[6]
+    pre = [[(j, gap(j, i)) for j in deps[i]] for i in range(n)]
+    post = [[] for _ in ops]
+    for i in range(n):
+        for j, d in pre[i]:
+            post[j].append((i, d))
+    tail = [o["x"][2] if o["k"] != "c" else 0.0 for o in ops]
+    keys = [key(o) for o in ops]
+    names = sorted(set(keys))
+
+    def place(seq, edges, rel):
+        st, busy = [0.0] * n, {e: [] for e in ENG}
+        for i in seq:
+            s, d, b = rel[i], ops[i]["d"], busy[ops[i]["e"]]
+            for j, w in edges[i]:
+                if st[j] + ops[j]["d"] + w > s:
+                    s = st[j] + ops[j]["d"] + w
+            k = len(b)
+            while k > 0 and b[k - 1][1] > s:
+                k -= 1
+            while k < len(b) and b[k][0] < s + d:
+                s = max(s, b[k][1])
+                k += 1
+            b.insert(k, (s, s + d))
+            st[i] = s
+        return st
+
+    def topo_order(pr, edges, back):
+        left, heap, seq = [len(e) for e in edges], [], []
+        heap = sorted((pr[i], i) for i in range(n) if left[i] == 0)
+        while heap:
+            i = heap.pop(0)[1]
+            seq.append(i)
+            new = False
+            for j, w in back[i]:
+                left[j] -= 1
+                if left[j] == 0:
+                    heap.append((pr[j], j))
+                    new = True
+            if new:
+                heap.sort()
+        return seq
+
+    zero = [0.0] * n
+    x, best, top = 12345, None, None
+    st = schedule(ops, deps, {})[2]
+    for r in range(ROUNDS + 1):
+        move = {}
+        for m in range(r % 5 if r else 0):
+            x = (x * 1103515245 + 12345) % 2147483648
+            k = names[(x >> 8) % len(names)]
+            x = (x * 1103515245 + 12345) % 2147483648
+            move[k] = (-6, -3, -2, -1, 1, 2, 3, 6)[(x >> 8) % 8] * 500.0
+        base = best[2] if best else st
+        if r % 2 == 0:
+            bk = place(topo_order([-base[i] - ops[i]["d"] - move.get(keys[i], 0.0) for i in range(n)], post, pre), post, tail)
+            pr = [-bk[i] - ops[i]["d"] - ops[i].get("b", 0.0) for i in range(n)]
+        else:
+            pr = [base[i] + move.get(keys[i], 0.0) - ops[i].get("b", 0.0) for i in range(n)]
+        fw = place(topo_order(pr, pre, post), pre, zero)
+        order = sorted(range(n), key=lambda i: (fw[i], i))
+        t = [replay(o, order, deps, c) for o, c in zip(vs, COSTS)]
+        if best is None or sum(t) <= sum(best[0]) + SLACK * (1.0 - r / (0.8 * ROUNDS + 1)) * (x % 1000) / 1000.0 or sum(t) <= sum(best[0]):
+            best = (t, order, fw)
+        if top is None or sum(t) < sum(top[0]):
+            top = best = (t, order, fw)
+    return top[1], top[0], top[2]
+
+
+def schedule(ops, deps, TUNE):
+    n = len(ops)
+    HOP = COSTS[0][5]
+    lat = [o["x"][2] if o["k"] != "c" else HOP for o in ops]
+    succ = [[] for _ in ops]
+    for i in range(n):
+        for j in deps[i]:
+            succ[j].append(i)
+    pr = [0.0] * n
+    nxt = {}
+    for i in range(n - 1, -1, -1):
+        pr[i] = ops[i]["d"] + lat[i] + max([pr[s] for s in succ[i]] + [0.0])
+        tag = (ops[i]["e"], CHAIN.get(ops[i]["w"][0][0] if ops[i]["w"] else ""))
+        if tag[1]:
+            pr[i] = max(pr[i], ops[i]["d"] + nxt.get(tag, 0.0))
+            nxt[tag] = pr[i]
+    for i in range(n):
+        pr[i] += ops[i].get("b", 0.0) + TUNE.get(key(ops[i]), 0.0)
+    left = [len(d) for d in deps]
+    rdy = [0.0] * n
+    free = {e: 0.0 for e in ENG}
+    cand = [i for i in range(n) if left[i] == 0]
+    order, start = [], [0.0] * n
+    while cand:
+        t0 = min(max(rdy[i], free[ops[i]["e"]]) for i in cand)
+        e = [ops[i]["e"] for i in cand if max(rdy[i], free[ops[i]["e"]]) == t0][0]
+        mine = [i for i in cand if ops[i]["e"] == e]
+        now = [i for i in mine if rdy[i] <= t0 + 60]
+        i = max(now, key=lambda x: (pr[x], -x))
+        soon = [x for x in mine if rdy[x] < t0 + 0.5 * ops[i]["d"] and pr[x] > pr[i] + ops[i]["d"]]
+        if soon:
+            i = min(soon, key=lambda x: (rdy[x], -pr[x]))
+        cand.remove(i)
+        start[i] = max(rdy[i], free[e])
+        free[e] = start[i] + ops[i]["d"]
+        order.append(i)
+        for s in succ[i]:
+            same = ops[s]["e"] == e and ops[i]["k"] == "c"
+            rdy[s] = max(rdy[s], free[e] + ((0 if e == "P" else 40) if same else lat[i]))
+            left[s] -= 1
+            if left[s] == 0:
+                cand.append(s)
+    return order, deps, start
+
+
+def emit(g, T, ops, order, deps):
+    Q = {"V": g.vector, "S": g.scalar, "P": g.tensor, "G": g, "Y": g.sync}
+    pos, cnt = {}, {e: 0 for e in ENG}
+    clock = {e: {} for e in ENG}
+    done, waits, need = {}, {}, set()
+    for i in order:
+        o = ops[i]
+        e = o["e"]
+        ck = clock[e]
+        w = []
+        for j in sorted(deps[i], key=lambda x: -pos[x][1]):
+            d = ops[j]
+            key, val = (d["e"], pos[j][0]) if d["k"] == "c" else (j, 1)
+            if d["k"] == "c" and d["e"] == "P" and e == "P":
+                continue
+            if ck.get(key, 0) >= val:
+                continue
+            w.append(j)
+            need.add(j)
+            ck[key] = val
+            if d["k"] != "rem":
+                for k2, v2 in done[j].items():
+                    if ck.get(k2, 0) < v2:
+                        ck[k2] = v2
+        waits[i] = w
+        cnt[e] += 1
+        pos[i] = (cnt[e], len(pos))
+        done[i] = dict(ck)
+    num, tot, sent, dmas = {}, {e: 0 for e in ENG}, 0, []
+    for i in order:
+        o = ops[i]
+        q = Q[o["e"]]
+        for j in waits[i]:
+            d = ops[j]
+            if d["k"] == "c":
+                q.wait_ge(T.sem["e" + d["e"]], num[j])
+            else:
+                q.wait_ge(d["x"][0], d["x"][1])
+        r = o["fn"]()
+        if o["k"] == "c":
+            if i in need:
+                tot[o["e"]] += 1
+                num[i] = tot[o["e"]]
+                r.then_inc(T.sem["e" + o["e"]], 1)
+        else:
+            if i not in need:
+                dmas.append(o)
+            if o["k"] == "rem":
+                sent += o["x"][1]
+    g.wait_ge(T.sem.sent, sent)
+    for o in dmas:
+        Q[o["e"]].wait_ge(o["x"][0], o["x"][1])
+
+
+def rank_program(g, core, T, topo):
+    if T.rank_of(core) is None:
+        return
+    if not PLAN:
+        PLAN.append(search(g, T, core, topo)[0])
+    ops = build(g, T, core, topo, COSTS[0])
+    emit(g, T, ops, PLAN[0], depend(ops))

@@ -1,22 +1,22 @@
 from concourse.bass import DstId, RemoteDMATransfer
-from concourse.mybir import AluOpType as OP, AxisListType, ActivationFunctionType as AF
+from concourse.mybir import AluOpType as OP, ActivationFunctionType as AF
 
 NV = 4
-CH = 64
-NCH = 256 // CH
-L2S = (1, 2, 3)
-XV = (0, 0, 32, 32)
-B2, B3 = ("E0", "K1", "K0", "K1"), ("E1", "E0", "E1", "E0")
-CHAIN = {"G": 1, "Ab": 1, "GF0": 1, "GF1": 1, "GF2": 1, "GH0": 3, "GH1": 3, "GH2": 3, "GL0": 2, "GL1": 2, "GL2": 2}
-EARLY = False
-L2G = (1, 2, 3)
-NB = (("K0", "K0"), ("D0", "D1"))
-UFIRST = True
-BZ, BU = 2500.0, 0.0
+ID = 256
+DIR, PP = ID + 4096, 6664
+WW = ID + PP + 128
+L2_FIRST = ((("V", 0, 64),), (("S", 64, 128),), (("S", 128, 192),), (("S", 192, 256),))
+L2_LATER = ((("V", 0, 64),), (("S", 64, 96), ("S", 96, 128)), (("S", 128, 160), ("S", 160, 192)), (("S", 192, 224), ("S", 224, 256)))
+AHEAD = 3
+PIECE = 32
+L3V = ((64, 64, 64, 64), (64, 64, 64, 64), (64, 64, 64, 64), (64, 64, 64, 64))
+XV = ((0, 0, 0, 0), (0, 0, 0, 0), (0, 0, 0, 0), (0, 0, 0, 0))
+START, PERIOD = 10.0, 21.0
+WHEN = {"thr": 3.0, "l30": 0.0, "l31": 2.7, "l32": 5.3, "l33": 7.4, "l22": 0.3, "pd1": 4.5, "on": 3.5, "g0": 2.9, "g1": 5.5, "g2": 8.5,
+        "g3": 10.5, "e0": 6.0, "t0": 8.5, "n0": 9.8, "e1": 12.0, "x0": 14.5, "ptr": 11.5, "l1": 12.5, "rows": 10.0, "l20": 13.5,
+        "l21": 18.0, "ed": 15.0, "t1": 17.5, "n1": 18.8, "x1": 22.6, "dir": 6.0, "top": 4.0, "out": 20.0}
+WHEN0 = {"f0": -2.0, "f1": -2.0, "f2": -0.5, "f3": 1.0, "rows0": 1.0, "ed0": 4.0}
 PLAN = []
-SEQ = "20 21 30 22 31 23 32 33"
-TAIL = ((0, 128), (128, 192), (192, 256))
-WW = 6664
 f32, bf, f16, i32, u16 = "float32", "bfloat16", "float16", "int32", "uint16"
 
 
@@ -25,45 +25,47 @@ def _sb(n, d):
 
 
 SCRATCH = {
-    "W": _sb(WW, f32), "X": _sb(4096, bf), "G": _sb(4096, bf), "Ab": _sb(4096, bf),
-    "rv": _sb(1024, i32), "rp": _sb(1024, i32), "vni": _sb(16, i32), "pni": _sb(16, i32),
-    "wti": _sb(1, i32), "thi": _sb(1, i32),
-    "GL0": _sb(1024, f16), "GL1": _sb(1024, f16), "GL2": _sb(1024, f16), "GF0": _sb(1024, f32), "GF1": _sb(1024, f32),
-    "GF2": _sb(1024, f32), "GH0": _sb(1024, f16), "GH1": _sb(1024, f16), "GH2": _sb(1024, f16),
+    "W": _sb(WW, f32), "X": _sb(4096, bf), "G": _sb(4096, bf), "Ab": _sb([16, 256], bf),
+    "rv": _sb(1024, i32), "rp": _sb(1024, i32), "pv": _sb(32, i32), "wti": _sb(1, i32), "thi": _sb(1, i32),
+    "GL0": _sb(1024, f16), "GL1": _sb(1024, f16), "GL2": _sb(1024, f16), "GH": _sb(4096, f16),
+    "GF0": _sb(1024, f32), "GF1": _sb(1024, f32), "GF2": _sb(1024, f32), "GF3": _sb(1024, f32),
     "o1": _sb(16, u16), "o2": _sb(256, u16), "o3": _sb(256, u16), "o4": _sb(256, u16),
-    "os": _sb(32, u16), "on": _sb(16, u16), "ox": _sb(16, u16), "oc": _sb(16, u16),
-    "F1": _sb(2048, bf), "F1f": _sb(2048, f32), "F3": _sb(2048, bf), "mk": _sb(16, f32), "of": _sb(2, u16),
-    "Z16": _sb(144, bf), "Zw": _sb(144, bf), "Zk": _sb(144, bf),
-    "Id": _sb(128, bf), "In": _sb(128, bf), "I2": _sb(128, bf), "Ip": _sb(128, bf), "Im": _sb(128, bf),
-    "I3": _sb(128, bf), "Ik": _sb(128, bf), "Ia": _sb(128, bf), "Ib": _sb(128, bf), "Ic": _sb(128, bf), "Iq": _sb(128, bf),
-    "Bk": _sb(128, bf), "Bi": _sb(128, f32), "onef": _sb(128, f32), "oneb": _sb(256, bf), "m128": _sb(256, bf),
-    "F4": _sb(2048, bf), "mk2": _sb(16, f32), "rf": _sb(512, f32), "d0": _sb(256, f32),
-    "Jz": _sb(512, f16), "Jh": _sb(16, f16), "Jd": _sb(32, f32), "ji": _sb(16, i32),
+    "on": _sb(16, u16), "ox": _sb(16, u16), "oc": _sb(8, u16), "of": _sb(2, u16),
+    "F1": _sb(2048, bf), "F3": _sb(2048, bf), "mk": _sb(16, f32), "Zw": _sb(144, bf), "Zn": _sb(144, bf),
+    "Bk": _sb(128, bf), "Tri": _sb(128, bf), "Bi": _sb(128, f32), "sel": _sb(16, bf), "KC": _sb(256, f16), "TC": _sb(512, bf),
+    "oneb": _sb(512, bf), "onef": _sb(128, f32), "m128": _sb(128, bf), "d0": _sb(128, f32),
+    "jl": _sb(16, f32), "Jn": _sb(16, f32), "Jh": _sb(8, f16), "J": _sb(32, f32), "mo": _sb(256, f32),
     "pi": _sb(1, i32), "ci": _sb(4, i32), "cf": _sb(8, f32),
-    "E": _sb(4096, bf), "dsg": _sb(256, bf), "mm": _sb(256, f32),
-    "kU": _sb(256, f32), "sc": _sb(256, f32), "ohU": _sb(256, bf), "oh": _sb(256, bf), "t1": _sb(256, f32),
-    "ee": _sb(256, f32), "sg": _sb(256, bf), "Q": _sb(512, f32), "nr": _sb(256, f32), "acc": _sb(4, f32),
-    "thr": _sb(1, f32), "ai": _sb(2, i32), "xs": _sb(256, bf), "xr": _sb(256, bf),
-    "ui": _sb(64, i32), "uf": _sb(64, f32), "lh": _sb(32, f16), "vnr": _sb(256, f16), "dl": _sb(64, f32),
+    "E": _sb([16, 256], bf), "dsg": _sb(256, bf), "rf": _sb(512, f32),
+    "sc": _sb(256, f32), "ky": _sb(256, f32), "oh": _sb(256, bf), "sg": _sb(256, bf), "es": _sb(256, f32), "rr": _sb(128, f32),
+    "eqN": _sb(256, bf), "xs": _sb(256, bf), "xr": _sb(256, bf), "ee": _sb(128, f32), "tov": _sb(256, f32), "top": _sb(256, f32),
+    "acc": _sb(2, f32), "thr": _sb(1, f32), "ai": _sb(2, i32), "ui": _sb(64, i32), "uf": _sb(32, f32), "lv": _sb(16, f16),
+    "dl": _sb(96, f32), "lq": _sb([3, 16], f16),
     "OV": _sb(1280, f32), "OPD": _sb(1280, f32), "OX": _sb(1024, f32), "OVP": _sb(256, f32),
 }
+SCALED = (("Id", 1.0), ("In", -1.0), ("I3", 3072.0), ("I4", 4096.0), ("Im4", -4096.0), ("Ia", 64.0), ("Ic", 262144.0), ("Iq", 512.0))
+for _n, _c in SCALED:
+    SCRATCH[_n] = _sb(128, bf)
 for _t in range(NV):
     SCRATCH["zz%d" % _t] = _sb(256, bf)
     SCRATCH["zn%d" % _t] = _sb(256, bf)
-    SCRATCH["rw%d" % _t] = _sb(512, f16)
     SCRATCH["ls%d" % _t] = _sb(64, f32)
     SCRATCH["lo%d" % _t] = _sb(64, f32)
-    SCRATCH["vr%d" % _t] = _sb(256, f16)
-PS = ["D0", "D1", "E0", "E1", "K0", "K1", "PV", "M"]
+    SCRATCH["lh%d" % _t] = _sb([3, 16], f16)
+    SCRATCH["rw%d" % _t] = _sb(512, f16)
+    SCRATCH["os%d" % _t] = _sb(32, u16)
+PS = ["D0", "D1", "E0", "E1", "K", "T", "N", "M"]
 for _n in PS:
     SCRATCH[_n] = ("psum", [128, 512], f32)
 ENG = "VSPGY"
 NDMA = 24
-SEMAPHORES = ["eV", "eS", "eP", "eG", "sent"] + ["d%d" % i for i in range(NDMA)] + ["a%d" % i for i in range(12)]
+SEMAPHORES = ["eV", "eS", "eP", "eG", "sent"] + ["d%d" % i for i in range(NDMA)] + ["a%d" % i for i in range(9)]
 
-COSTS = [(1.04, 0.52, 60.0, 1.56, 3.8, 110.0, 40.0), (1.04, 0.52, 60.0, 1.1, 2.0, 110.0, 40.0), (1.04, 0.52, 60.0, 2.0, 5.5, 110.0, 40.0),
-         (1.04, 0.42, 30.0, 1.56, 3.8, 60.0, 20.0), (1.04, 0.7, 60.0, 1.56, 3.8, 110.0, 40.0), (1.04, 0.52, 60.0, 1.56, 3.8, 250.0, 120.0)]
-ROUNDS, SLACK = 5000, 1500.0
+COSTS = [(0.92, 0.46, 40.0, 1.56, 3.8, 120.0, 50.0, 3000.0), (0.92, 0.46, 40.0, 1.1, 2.0, 120.0, 50.0, 3000.0),
+         (0.92, 0.46, 40.0, 2.0, 5.5, 120.0, 50.0, 3000.0), (1.15, 0.58, 40.0, 1.56, 3.8, 120.0, 50.0, 2500.0),
+         (0.92, 0.46, 60.0, 1.56, 3.8, 250.0, 100.0, 4500.0)]
+ROUNDS, SLACK = 100, 1500.0
+ANNEAL = ((0, 4), 80000, 1500.0)
 
 
 def build(g, T, core, topo, C):
@@ -74,21 +76,15 @@ def build(g, T, core, topo, C):
     rid, pid, _ = topo.addr(nxt)
     engs = topo.engines(core, nxt)
     V, S, P = g.vector, g.scalar, g.tensor
-    nd, na = [0], [0]
+    nd, na, now = [0], [0], [0.0]
 
     def A(name, lo=None, hi=None, step=None):
         t = T[name]
-        n = 1
-        for s in t.shape[1:]:
-            n *= s
         if lo is None:
-            return (t[:], name, 0, n, n)
+            return (t[:], name, 0, t.shape[1], t.shape[1])
         if step is None:
             return (t[:, lo:hi], name, lo, hi, hi - lo)
         return (t[:, lo:hi:step], name, lo, hi, len(range(lo, hi, step)))
-
-    def V3(name, ap, n):
-        return (ap, name, 0, 1 << 20, n)
 
     def IND(win, off):
         return (win[0].indirect(off[0]), win[1], win[2], win[3], 16 * off[4], off)
@@ -104,7 +100,11 @@ def build(g, T, core, topo, C):
             wr.append(a[1:4])
             if len(a) > 5:
                 rd.append(a[5][1:4])
-        ops.append({"e": eng, "fn": fn, "r": rd, "w": wr, "d": dur, "k": kind, "x": extra})
+        ops.append({"e": eng, "fn": fn, "r": rd, "w": wr, "d": dur, "k": kind, "x": extra, "at": now[0]})
+        now[0] += dur + 100.0
+
+    def at(t, name):
+        now[0] = 1000.0 * (START + PERIOD * t + (WHEN0 if t == 0 and name in WHEN0 else WHEN)[name])
 
     def ap(a):
         return a[0] if isinstance(a, tuple) else a
@@ -114,10 +114,10 @@ def build(g, T, core, topo, C):
 
     def vd(o, i, rate):
         if len(o) > 5:
-            return FIX + SCA * CY * o[4]
+            return 50 + SCA * CY * o[4]
         if len(i) > 5:
-            return FIX + GA * CY * i[4]
-        return FIX + CY * max(40, rate * o[4])
+            return 50 + GA * CY * i[4]
+        return FIX + CY * max(48, rate * o[4])
 
     def cp(o, i):
         add("V", lambda: V.tensor_copy(o[0], i[0]), [o], [i], vd(o, i, 0.5 if two(o) and two(i) else 1))
@@ -135,15 +135,13 @@ def build(g, T, core, topo, C):
     def ms(o, c):
         add("V", lambda: V.memset(o[0], c), [o], [], vd(o, o, 0.5 if two(o) else 1))
 
-    def tr(o, i):
-        add("V", lambda: V.transpose(o[0], i[0]), [o], [i], vd(o, i, 0.5 if two(o) else 1))
-
     def act(o, i, f, bias=0.0, scale=1.0, acc=None):
         if acc is None:
             fn = lambda: S.activation(o[0], i[0], f, bias=ap(bias), scale=ap(scale))
         else:
             fn = lambda: S.activation(o[0], i[0], f, bias=ap(bias), scale=ap(scale), accum_out=acc[0])
-        add("S", fn, [o] + ([acc] if acc else []), [i, bias, scale], FIX + CY * (GA if len(i) > 5 else 1) * max(40, i[4]))
+        add("S", fn, [o] + ([acc] if acc else []), [i, bias, scale],
+            65 + GA * CY * i[4] if len(i) > 5 else FIX + CY * max(48, i[4]) + (20 if acc else 0))
 
     def mm(lst):
         def fn():
@@ -151,21 +149,24 @@ def build(g, T, core, topo, C):
             for o, l, x, st, sp in lst:
                 r = P.matmul(o[0], l[0], x[0], st, sp)
             return r
-        d = sum(max(64, x[4]) * (4 if SCRATCH[x[1]][2] == f32 else 1) * PCY + 4 for o, l, x, st, sp in lst)
+        d = sum(max(64, x[4]) * (4 if SCRATCH[x[1]][2] == f32 else 1) * PCY + 3 for o, l, x, st, sp in lst)
         add("P", fn, [m[0] for m in lst], [m[1] for m in lst] + [m[2] for m in lst], d + 30)
 
-    def grp(lst):
-        mm([(o, l, x, n == 0, n == len(lst) - 1) for n, (o, l, x) in enumerate(lst)])
+    def grp(lst, start=True, stop=True):
+        mm([(o, l, x, start and n == 0, stop and n == len(lst) - 1) for n, (o, l, x) in enumerate(lst)])
 
     def iota(o, pat, base, cm):
         if SCRATCH[o[1]][2] == i32:
             fn = lambda: g.iota(o[0], pat, base, cm)
         else:
             fn = lambda: g.iota(o[0], pat, base, cm, allow_small_or_imprecise_dtypes=True)
-        add("G", fn, [o], [], 160 + 2 * CY * o[4])
+        add("G", fn, [o], [], 150 + 2 * CY * o[4])
 
-    def narrow(o, i):
-        add("G", lambda: g.affine_select(o[0], i[0], [[0, o[4]]], OP.is_ge, 0.0, 0, 0), [o], [i], 210 + 2 * CY * o[4])
+    def select(o, i, pat, op, base, cm):
+        add("G", lambda: g.affine_select(o[0], i[0], pat, op, 0.0, base, cm), [o], [i], 190 + 2 * CY * o[4])
+
+    def gcopy(o, i):
+        select(o, i, [[0, o[4]]], OP.is_ge, 0, 0)
 
     def dma(q, o, i, nbytes, slow=False):
         sem = T.sem["d%d" % nd[0]]
@@ -175,317 +176,349 @@ def build(g, T, core, topo, C):
             fn = lambda: Q.dma_start(ap(o), ap(i), allow_slow_non_contiguous=True).then_inc(sem, 16)
         else:
             fn = lambda: Q.dma_start(ap(o), ap(i)).then_inc(sem, 16)
-        add(q, fn, [o] if isinstance(o, tuple) else [], [i], 1000 if q == "G" else 100, "dma", (sem, 16, 1800 + nbytes / 200.0))
+        add(q, fn, [o] if isinstance(o, tuple) else [], [i], 1000 if q == "G" else 80, "dma", (sem, 16, 1500 + nbytes / 250.0))
 
-    def send(pairs, per):
+    def send(o, i):
         sem = T.sem["a%d" % na[0]]
         na[0] += 1
-        trs = []
-        for n, (o, i) in enumerate(pairs):
-            m = 0
-            for e in engs[n * per:(n + 1) * per]:
-                m |= 1 << e
-            trs.append(RemoteDMATransfer(dst_ids=[DstId(rid=rid, pnc=pid)], dma_engine_mask=m, remote_sem=sem, src=i[0], dst=o[0]))
-        if len(pairs) == 1:
-            fn = lambda: g.remote_dma(pairs[0][0][0], pairs[0][1][0], sem, T.sem.sent, pid, rid, m)
-        else:
-            fn = lambda: g.remote_dma_fused(trs, local_sem=T.sem.sent)
-        add("G", fn, [p[0] for p in pairs], [p[1] for p in pairs], 800, "rem", (sem, per * len(pairs), 3500))
+        m = 0
+        for e in engs[:4]:
+            m |= 1 << e
+        add("G", lambda: g.remote_dma(o[0], i[0], sem, T.sem.sent, pid, rid, m), [o], [i], 800, "rem", (sem, 4, C[7]))
 
-    ID, ABS, SIGN, RELU = AF.Identity, AF.Abs, AF.Sign, AF.Relu
+    IDN, ABS, SIGN = AF.Identity, AF.Abs, AF.Sign
     F = lambda n, k: A(n, 128 * k, 128 * k + 128)
     Z = lambda n, k: A(n, 15 - k, 143 - k)
+    R = lambda a, b, st=None: A("W", ID + 1 + a, ID + 1 + b, st)
+    VDw = lambda a, b: A("W", DIR + 2 + 2 * a, DIR + 1 + 2 * b, 2)
+    PDw = lambda a, b: A("W", DIR + 1 + 2 * a, DIR + 2 * b, 2)
     col = lambda k: A("cf", k, k + 1)
+    LH = lambda t, a, b: (T["lh%d" % t][:, a:b, :], "lh%d" % t, 16 * a, 16 * b, 16 * (b - a))
+    LH1 = lambda t, a: (T["lh%d" % t][:, a, :], "lh%d" % t, 16 * a, 16 * a + 16, 16)
 
-    first = [len(ops)]
     dma("Y", A("rv", 0, 512), T.vdir[:, 0:512], 262144)
-    dma("S", A("rp", 0, 512), T.pdir[:, 0:512], 2 * 262144)
-    dma("Y", A("rv", 512, 1024), T.vdir[:, 512:1024], 3 * 262144)
-    dma("S", A("rp", 512, 1024), T.pdir[:, 512:1024], 4 * 262144)
-    dma("Y", A("vni"), T.vn[:], 4 * 262144)
-    dma("S", A("pni"), T.pn[:], 4 * 262144)
+    dma("Y", A("rv", 512, 1024), T.vdir[:, 512:1024], 2 * 262144)
+    dma("Y", A("pv", 16, 32), T.vn[:], 2 * 262144)
+    dma("Y", A("rp", 0, 512), T.pdir[:, 0:512], 3 * 262144)
+    dma("Y", A("rp", 512, 1024), T.pdir[:, 512:1024], 4 * 262144)
+    dma("Y", A("pv", 0, 16), T.pn[:], 4 * 262144)
     dma("Y", A("zz0"), T.z[:], 4 * 262144)
     dma("Y", A("X"), T.xl[:], 8 * 262144)
+    iota(R(0, 256), [[1, 256]], 0, 0)
     iota(A("pi"), [[0, 1]], 0, 1)
-    iota(A("W", 0, 512), [[1, 512]], 4095, 0)
-    for n in range(first[0], len(ops)):
-        ops[n]["b"] = 1.0e6 * (20 - n)
-    iota(A("ji"), [[16, 16]], 0, 0)
+    for n, o in enumerate(ops):
+        o["b"] = 1.0e6 * (20 - n)
+    iota(R(3072, 4096), [[1, 1024]], 3072, 0)
     iota(A("Bi"), [[1, 8], [0, 16]], 0, 0)
-    ops[-1]["b"] = 1.0e5
-    iota(A("W", 3072, 4097), [[1, 1025]], 4095 + 3072, 0)
-    dma("G", A("wti"), T.wt[:], 512, True)
-    dma("G", A("thi"), T.th[:], 512, True)
+    ms(A("oneb"), 1.0)
     ms(A("F1"), 0.0)
+    ts(R(256, 512), R(0, 256), 256.0, OP.add)
+    ts(R(512, 1024), R(0, 512), 512.0, OP.add)
+    act(R(1024, 2048), R(0, 1024), IDN, bias=1024.0)
+    ts(R(2048, 2560), R(0, 512), 2048.0, OP.add)
+    act(R(2560, 3072), R(0, 512), IDN, bias=2560.0)
     cp(col(0), A("pi"))
     ts(A("ci", 0, 1), A("pi"), 15, OP.bitwise_and)
     ts(A("ci", 1, 2), A("pi"), 4, OP.arith_shift_right)
     cp(A("cf", 1, 3), A("ci", 0, 2))
+    ts(A("Id"), R(0, 128), col(0), OP.is_equal)
+    for n, c in SCALED[1:]:
+        act(A(n), A("Id"), IDN, scale=c)
     ts(A("of", 0, 1), col(1), 128.0, OP.mult, col(0), OP.add)
-    ts(col(7), col(2), 16.0, OP.mult, 4095.0 + 15.0, OP.add)
-    ts(A("mk"), A("W", 0, 16), -4095.0, OP.add, col(1), OP.is_equal)
+    ts(A("mk"), R(0, 16), col(1), OP.is_equal)
     cp(IND(A("F1"), A("of", 0, 1)), A("mk"))
-    for n in range(len(ops) - 9, len(ops)):
-        ops[n]["b"] = 1.0e5
-    ts(A("W", 512, 1024), A("W", 0, 512), 512.0, OP.add)
-    ts(A("W", 1024, 2048), A("W", 0, 1024), 1024.0, OP.add)
-    for b in (2048, 2560):
-        act(A("W", b, b + 512), A("W", 0, 512), ID, bias=float(b))
-    if [c for c in L2S if c not in L2G]:
+    for raw, win, bias, banks in (("rv", VDw, -4096.0, ("D0", "D1")), ("rp", PDw, -4095.0, ("T", "N"))):
         for h in range(2):
-            act(A("F1f", 1024 * h, 1024 * h + 1024), A("F1", 1024 * h, 1024 * h + 1024), ID)
-    ts(A("Id"), A("W", 0, 128), -4095.0, OP.add, col(0), OP.is_equal)
-    for n, c in (("In", -1.0), ("I2", 2.0), ("Ip", 8192.0), ("Im", -8192.0), ("I3", 3072.0), ("Ia", 64.0), ("Ib", 4096.0),
-                 ("Ic", 262144.0), ("Iq", 1024.0)):
-        act(A(n), A("Id"), ID, scale=c)
-    act(A("Ik"), A("Id"), ID, scale=col(1))
-    ms(A("oneb"), 1.0)
+            a, b = 512 * h, 512 * h + 512
+            ts(A(banks[h]), A(raw, a, b), 2.0, OP.mult, bias, OP.add)
+            tt(win(a, b), A(raw, a, b), A(banks[h]), OP.max)
+    ts(A("ls0", 16, 32), A("pv", 16, 32), 2.0, OP.mult)
+    ts(A("ls0", 0, 16), A("pv", 0, 16), 2.0, OP.mult, -1.0, OP.add)
+    now[0] = 1.0e6
+    for q in range(4):
+        select(A("F3", 512 * q, 512 * q + 512), A("oneb"), [[-1, 4], [-16, 8], [0, 16]], OP.is_equal, -4 * q, 1)
+    dma("G", A("wti"), T.wt[:], 512, True)
+    dma("G", A("thi"), T.th[:], 512, True)
+    act(col(4), col(2), IDN, scale=16.0, bias=15.0)
+    cp(col(5), A("wti"))
+    ts(col(6), A("thi"), -16.0, OP.mult)
+    ts(A("Zw"), R(0, 144), col(4), OP.is_equal, col(5), OP.mult)
+    ts(A("Zn"), R(0, 144), col(4), OP.is_equal, col(1), OP.mult)
+    for b in (0, 8):
+        ts(A("sel", b, b + 8), R(0, 8), col(2), OP.is_equal, 16.0, OP.mult)
+    ts(A("KC", 0, 128), A("Id"), col(1), OP.mult)
+    ts(A("KC", 128, 256), A("Id"), col(6), OP.mult)
+    iota(A("TC", 0, 256), [[2048, 2], [0, 128]], -4096, 0)
+    gcopy(A("TC", 256, 512), A("oneb", 0, 256))
+    ts(A("Bk"), A("Bi"), col(2), OP.is_equal)
+    select(A("Tri"), A("Bk"), [[1, 128]], OP.is_gt, 0, -1)
     ms(A("onef"), 1.0)
     ms(A("m128"), -128.0)
-    ts(A("Jz", 0, 256), A("W", 0, 256), -4095.0, OP.add, 16.0, OP.mult)
-    ts(A("Jz", 256, 512), A("oneb"), 0.0, OP.mult)
-    ts(A("oc"), A("ji"), 15.0, OP.add)
-    ts(A("Jd", 0, 16), A("ji"), col(1), OP.add, 1024.0, OP.add)
-    ts(A("Jd", 16, 32), A("ji"), col(1), OP.add, 1023.5, OP.add)
-    ts(A("Jh"), A("ji"), col(1), OP.add, 16.0, OP.mult)
-    ts(A("Jh", 12, 16), A("Jh", 12, 16), -3072.0, OP.add)
-    ts(A("Z16"), A("W", 0, 144), col(7), OP.is_equal, 16.0, OP.mult)
-    ts(A("Zk"), A("W", 0, 144), col(7), OP.is_equal, col(1), OP.mult)
-    cp(col(5), A("wti"))
-    ts(A("Zw"), A("W", 0, 144), col(7), OP.is_equal, col(5), OP.mult)
-    ts(col(6), A("thi"), 16.0, OP.mult, -0.5, OP.add)
-    ts(A("Bk"), A("Bi"), col(2), OP.is_equal)
-    ops[-1]["b"] = 1.0e5
-    ts(A("mk2"), A("W", 0, 16), -4095.0, OP.add, col(1), OP.is_gt)
-    for s in range(16):
-        act(F("F4", s), A("Bk"), ID, scale=A("mk2", s, s + 1))
     ms(A("d0"), 0.0)
-    ms(A("d0", 0, 256, 16), 1.0e6)
-    for s in range(16):
-        act(F("F3", s), A("Bk"), ID, scale=A("mk", s, s + 1))
-    VDw, PDw = lambda a, b: A("W", 4098 + 2 * a, 4098 + 2 * b - 1, 2), lambda a, b: A("W", 4097 + 2 * a, 4097 + 2 * b - 1, 2)
-    for h in range(2):
-        ts(A("D0"), A("rv", 512 * h, 512 * h + 512), 4096.0, OP.max)
-        tt(VDw(512 * h, 512 * h + 512), A("rv", 512 * h, 512 * h + 512), A("D0"), OP.add)
-        ts(A("D1"), A("rp", 512 * h, 512 * h + 512), 1.0, OP.add, 4096.0, OP.max)
-        tt(PDw(512 * h, 512 * h + 512), A("rp", 512 * h, 512 * h + 512), A("D1"), OP.add)
-    cp(A("ls0", 0, 16), A("vni"))
-    ts(A("ls0", 16, 32), A("pni"), -0.5, OP.add)
-    cp(A("uf", 32, 48), A("pni"))
+    ms(A("d0", 0, 128, 16), 1.0e6)
+    ts(A("jl"), R(0, 256, 16), col(1), OP.add)
+    ts(A("oc"), R(0, 128, 16), 15.0, OP.add)
+    ts(A("Jh"), A("jl", 0, 8), 16.0, OP.mult)
+    act(A("Jn"), A("jl"), IDN, scale=16.0, bias=-2048.0)
+    act(A("J", 0, 16), A("jl"), IDN, scale=2.0, bias=2047.0 - 4096.0)
+    act(A("J", 16, 32), A("jl"), IDN, scale=2.0, bias=2048.0 - 4096.0)
+    act(A("W", ID + PP, WW), R(0, 128), IDN, scale=2.0, bias=-1.0 - ID)
+    ngl, ngf, ne = [0], [0], [0]
 
-    def torows(first):
-        grp(first + [(A("M", s, 512, 16), F("F3", s), A("lh")) for s in range(16)])
+    def rows(t):
+        cp(LH(t, 1, 3), A("ls%d" % t, 0, 32))
+        lo = 0 if t == 0 else 256
+        mm([(A("M", lo + s, 512, 16), F("F3", s), LH(t, 1, 3) if t == 0 else LH1(t, 2), True, True) for s in range(16)])
+        act(A("rf", lo, 512), A("M", lo, 512), IDN)
+        gcopy(A("rw%d" % t, lo, 512), A("rf", lo, 512))
 
-    def dups(row, lst, out):
+    def repeats(t, r0, l0, out):
         for c in range(16):
             n = 256 - 16 * c
-            ts(A("E", 256 * c, 256 * c + n), A(row[0], row[1] + 16 * c, row[1] + 256), A(lst[0], lst[1] + c, lst[1] + c + 1), OP.is_equal)
-        lst = [(A("M", 0, 256), F("F4", 0), A("oneb"))]
-        lst += [(A("M", 16 * c + 16, 256), A("Bk"), A("E", 256 * c + 16, 240 * c + 256)) for c in range(15)]
-        lst += [(A("M", s, 256, 16), F("F4", s), A("E", s, 4096, 256)) for s in range(1, 16)]
-        for k0 in (0, 6, 16):
-            mm([(o, l, x, n == 0, n == 30) for n, (o, l, x) in enumerate(lst)][k0:{0: 6, 6: 16, 16: 31}[k0]])
+            ts((T.E[:, c, 0:n], "E", 256 * c, 256 * c + n, n), A("rw%d" % t, r0 + 16 * c, r0 + 256), A("ls%d" % t, l0 + c, l0 + c + 1), OP.is_equal)
+        grp([(A("M", 0, 256), A("Tri"), (T.E[:, :, 0:16], "E", 0, 4096, 256))] +
+            [(A("M", 16 * c + 16, 256), A("Bk"), (T.E[:, c, 16:256 - 16 * c], "E", 256 * c, 256 * c + 256, 240 - 16 * c)) for c in range(15)])
         act(A("dsg"), A("M", 0, 256), SIGN)
         grp([(A("M", 256, 272), F("F1", s), A("dsg", s, 256, 16)) for s in range(16)])
         for b in (32, 48):
-            act(A(out, b, b + 16), A("M", 256, 272), ID, scale=2048.0, bias=-1.0)
+            act(A(out, b, b + 16), A("M", 256, 272), IDN, scale=4096.0)
 
-    cp(A("lh", 0, 16), A("vni"))
-    cp(A("lh", 16, 32), A("pni"))
-    mm([(A("M", s, 512, 16), F("F3", s), A("lh"), True, True) for s in range(16)])
-    act(A("rf"), A("M"), ID)
-    narrow(A("rw0"), A("rf"))
-    dups(("rw0", 256), ("uf", 32), "ls0")
-    ngl, ngf, ne = [0], [0], [0]
-
-    for t in range(NV):
-        last = t == NV - 1
-        zz, zn, rw, ls, lo, vr = ["%s%d" % (n, t) for n in ("zz", "zn", "rw", "ls", "lo", "vr")]
-        if t == 0:
-            thr = col(6)
+    def edits(t):
+        ls, lo = "ls%d" % t, "lo%d" % t
+        repeats(t, 256, 16, lo)
+        tt(A("dl", 0, 32), A(lo, 32, 64), A(ls, 32, 64), OP.max)
+        tt(A("dl", 32, 64), A("dl", 0, 32), A("J"), OP.add)
+        tt(A("dl", 64, 96), A(ls, 0, 32), A("dl", 32, 64), OP.max)
+        if t < NV - 1:
+            ts(A("os%d" % t), A("dl", 64, 96), 2.0, OP.add)
         else:
-            grp([(A("M", 0, 1), A("onef"), A("acc", c, c + 1)) for c in range(len(TAIL))])
-            ts(A("ai", 0, 1), A("M", 0, 1), -0.5, OP.mult, 16384.0, OP.add)
-            ts(A("ai", 1, 2), A("ai", 0, 1), 255, OP.bitwise_and)
-            ts(A("thr"), A("ai", 1, 2), 16.0, OP.mult, col(6), OP.add)
-            thr = A("thr")
-        ts(A("o1"), A(ls, 0, 16), 2.0, OP.mult, 2.0, OP.add)
-        for a, b in ((0, 128), (128, 256)):
-            ts(A("o2", a, b), IND(A("W", 4096, 6145), A("o1", a // 16, b // 16)), -4095.0, OP.add)
-        if last:
-            for h in range(2):
-                for n, win, bias in (("OV", VDw, -4096.0), ("OPD", PDw, -4095.5)):
-                    act(A(n, 512 * h, 512 * h + 512), win(512 * h, 512 * h + 512), ID, bias=-4096.0)
-                    act(A("K1"), win(512 * h, 512 * h + 512), RELU, bias=bias, scale=0.5)
-                    tt(A(n, 512 * h, 512 * h + 512), A(n, 512 * h, 512 * h + 512), A("K1"), OP.subtract)
-        def edits():
-            if t == 0 or not EARLY:
-                dups((rw, 0), (ls, 0), lo)
-            tt(A("dl", 0, 32), A(lo, 32, 64), A(ls, 32, 64), OP.max)
-            tt(A("dl", 32, 64), A("dl", 0, 32), A("Jd"), OP.min)
-            tt(A("dl", 0, 32), A("dl", 32, 64), A(ls, 0, 32), OP.max)
-            if last:
-                ts(A("os"), A("dl", 0, 32), 0.25, OP.add)
-            else:
-                ts(A("os"), A("dl", 0, 32), 2.0, OP.mult, 2.0, OP.add)
+            ts(A("os%d" % t), A("dl", 64, 96), 0.5, OP.mult, 0.25, OP.add)
 
-        if not UFIRST:
-            edits()
-        n0 = len(ops)
+    def entries(t, h, n):
+        win = A("W", DIR, ID + PP) if t < NV - 1 else A(("OPD", "OV")[n])
+        cp(IND(win, A("os%d" % t, 16 * n + 8 * h, 16 * n + 8 * h + 8)), A(("top", "tov")[n], 128 * h, 128 * h + 128))
+
+    def pointers(t):
+        win, os = A("W", DIR, ID + PP), "os%d" % t
+        ts(IND(win, A(os, 24, 32)), R(0, 128), 1.0, OP.mult, PP - 1.0, OP.add)
+        ts(IND(win, A(os, 8, 16)), R(0, 128), 2.0, OP.mult, -1.0 - ID, OP.add)
+
+    def look1(t):
+        ts(A("o1"), A("ls%d" % t, 16, 32), 2.0, OP.add)
+        for a, b in ((0, 64), (64, 256)) if t == 0 else ((0, 256),):
+            ts(A("o2", a, b), IND(A("W", DIR, DIR + 2056), A("o1", a // 16, b // 16)), 1.0, OP.add)
+
+    def bank():
+        ne[0] += 1
+        return "E%d" % (ne[0] % 2)
+
+    def look2(t, unit):
+        for eng, a, b in unit:
+            win = IND(A("W", ID, DIR + 2056 if t == 0 else WW), A("o2", a, b))
+            if eng == "V":
+                ts(A("GH", 16 * a, 16 * b), win, -2047.0, OP.add)
+            else:
+                gf = "GF%d" % (ngf[0] % 4)
+                ngf[0] += 1
+                act(A(gf, 0, 16 * (b - a)), win, IDN, bias=-2047.0)
+                for c in range(0, 16 * (b - a), 512):
+                    gcopy(A("GH", 16 * a + c, 16 * a + c + 512), A(gf, c, c + 512))
+        a, b, e = unit[0][1], unit[-1][2], bank()
+        grp([(A(e, 0, b - a), F("F1", k), A("GH", 16 * a + k, 16 * b, 16)) for k in range(16)])
+        ts(A("o3", a, b), A(e, 0, b - a), 2048.0 + ID, OP.add)
+
+    def look3(t, c):
+        a, b, e, gl = 64 * c, 64 * c + 64, bank(), "GL%d" % (ngl[0] % 3)
+        ngl[0] += 1
+        m = a + L3V[t][c]
+        if m > a:
+            ts(A(gl, 0, 16 * (m - a)), IND(A("W", 0, DIR + 2056), A("o3", a, m)), -2048.0, OP.add, 0.5, OP.mult)
+        for x in range(m, b, PIECE):
+            gf = "GF%d" % (ngf[0] % 4)
+            ngf[0] += 1
+            act(A(gf, 0, 16 * PIECE), IND(A("W", 0, DIR + 2056), A("o3", x, x + PIECE)), IDN, scale=0.5, bias=-1024.0)
+            for y in range(0, 16 * PIECE, 512):
+                gcopy(A(gl, 16 * (x - a) + y, 16 * (x - a) + y + 512), A(gf, y, y + 512))
+        grp([(A(e, 0, 64), A("I3"), A("oneb", 0, 64))] + [(A(e, 0, 64), F("F1", k), A(gl, k, 1024, 16)) for k in range(16)])
+        ts(A("mo", a, b), A(e, 0, 64), 4096.0, OP.is_lt, 1.0, OP.add)
+        tt(A("es", a, b), A(e, 0, 64), A("mo", a, b), OP.mult)
+        ts(A("o4", a, b), A("es", a, b), -4096.0, OP.add)
+
+    def lines(t, c):
+        a, b, h = 64 * c, 64 * c + 64, c // 2
+        m = a + XV[t][c]
+        if m > a:
+            cp(A("G", 16 * a, 16 * m), IND(A("X"), A("o4", a, m)))
+        if m < b:
+            act(A("G", 16 * m, 16 * b), IND(A("X"), A("o4", m, b)), IDN)
+        if c % 2:
+            grp([(A("K", 0, 256), A("oneb", 0, 128), A("KC"))], stop=False)
+        for hh in range(2):
+            d, lst = "D%d" % hh, []
+            for kk in range(8):
+                o = A(d, 64 * kk, 64 * kk + 64)
+                lst += [(o, A("Id"), A("G", 16 * a + 8 * hh + kk, 16 * b, 16), True, False), (o, A("In"), A("zz%d" % t, a, b), False, True)]
+            mm(lst)
+            act((T.Ab[:, 8 * hh:8 * hh + 8, a:b], "Ab", 256 * hh + a, 256 * hh + b, 512), A(d), ABS)
+            if c % 2:
+                grp([(A("K", k, 256, 16), (T.Ab[:, k, 128 * h:128 * h + 128], "Ab", 256 * hh + 128 * h, 256 * hh + 128 * h + 128, 128), A("sel"))
+                     for k in range(8 * hh, 8 * hh + 8)], start=False, stop=hh == 1)
+
+    def early(t, h):
+        n = "lh%d" % t if t < NV - 1 else "lq"
+        lh = (T[n][:, :, 8 * h:8 * h + 8], n, 0, 48, 24)
+        grp([(A("T"), A("Id"), A("TC"))] + [(A("T", 128 + s, 512, 16), F("F3", s), lh) for s in range(16)], stop=False)
+
+    def tail(t, h, thr):
+        a, b, last = 128 * h, 128 * h + 128, t == NV - 1
+        o, d0, d1 = A("sc", a, b), A("d0"), A("ky", a, b)
+        act(d1, A("K", 0, 128), IDN)
+        add("V", lambda: V.tensor_tensor_scan(o[0], d0[0], d1[0], 0.0, OP.add, OP.min), [o], [d0, d1], FIX + CY * 128)
+        act(A("sg", a, b), A("K", 128, 256), SIGN, bias=thr, scale=-1.0, acc=None if last else A("acc", h, h + 1))
+        tt(A("oh", a, b), IND(A("sc", a, b), A("oc")), d1, OP.is_equal)
+        grp([(A("T", 256, 384), A("sg", a, b), A("Im4")), (A("T", 384, 512), A("sg", a, b), A("I4"))], start=False, stop=False)
+        grp([(A("T", 0, 128), A("oh", a, b), A("Im4")), (A("T", 128, 256), A("oh", a, b), A("I4"))], start=False)
+        grp([(A("N", 0, 128), A("oh", a, b), A("Id"))])
+        act(A("eqN", a, b), A("N", 0, 128), IDN)
+        ee = A("W", 0, ID, 2) if h and not last else A("ee")
+        tt(A("rr"), A("es", a, b), A("T", 0, 128), OP.add)
+        tt(ee, A("rr"), A("T", 128, 256), OP.max)
+        tt(A("tov", a, b), ee, A("T", 256, 384), OP.max)
+        entries(t, h, 1)
+        tt(A("top", a, b), ee, A("T", 384, 512), OP.max)
+        if last or not h:
+            entries(t, h, 0)
+
+    def nearest(t, h):
+        a, b, zz, zn = 128 * h, 128 * h + 128, "zz%d" % t, "zn%d" % t
+        grp([(A("N", 256, 264), A("Id"), A("Jh"))] + [(A("N", 256, 264), Z("Zn", s), A("eqN", a + s, b, 16)) for s in range(16)])
+        cp(A("ox", 8 * h, 8 * h + 8), A("N", 256, 264))
+        act(A("xs", a, b), IND(A("G", 16 * a, 16 * b), A("ox", 8 * h, 8 * h + 8)), IDN)
+        mm([(A("N", 0, 128), A("Id"), A("xs", a, b), True, False), (A("N", 0, 128), A("In"), A(zz, a, b), False, True),
+            (A("N", 128, 256), A("Id"), A("xs", a, b), True, False), (A("N", 128, 256), A("Id"), A(zz, a, b), False, True)])
+        if t < NV - 1:
+            act(A(zn, a, b), A("N", 0, 128), ABS)
+            send(A("zz%d" % (t + 1), a, b), A(zn, a, b))
+        act(A("xr", a, b), A("N", 128, 256), IDN, bias=127.75, scale=0.5)
+        if t == NV - 1:
+            act(A(zn, a, b), A("N", 0, 128), ABS)
+
+    def newline(t, h):
+        win = A("X", 2048 * h, 2048 * h + 2048) if t == NV - 1 else A("X")
+        tt(IND(win, A("on", 8 * h, 8 * h + 8)), A("xr", 128 * h, 128 * h + 128), A("m128"), OP.add)
+
+    def onward(t):
+        zz, ls, lo = "zz%d" % t, "ls%d" % t, "lo%d" % t
         grp([(A("M", 0, 16), Z("Zw", s), A(zz, s, 256, 16)) for s in range(16)])
         cp(A("ui", 0, 16), A("M", 0, 16))
         ts(A("ui", 16, 32), A("ui", 0, 16), 4095, OP.bitwise_and)
         ts(A("ui", 32, 48), A("ui", 0, 16), 15, OP.bitwise_and)
         tt(A("uf", 0, 16), A("ui", 16, 32), A("ui", 16, 32), OP.mult)
-        act(A("uf", 16, 32), A(ls, 0, 16), ID, scale=1184.0, bias=-1184.0 * 1024)
+        act(A("uf", 16, 32), A(ls, 16, 32), IDN, scale=592.0, bias=-1184.0 * 1024)
         tt(A("ui", 0, 16), A("uf", 0, 16), A("uf", 16, 32), OP.add)
         ts(A("ui", 48, 64), A("ui", 0, 16), 5, OP.arith_shift_right, 1023, OP.bitwise_and)
-        cp(A("lh"), A("ui", 32, 64))
-        grp([(A("M", 0, 32), A("Id"), A("lh")), (A("M", 0, 16), A("Id"), A("Jh"))])
-        cp(A("on"), A("M", 0, 16))
-        if not last:
-            act(A(lo, 0, 16), A("M", 16, 32), ID)
-        if last:
-            torows([(A("M"), A("Id"), A("Jz")), (A("M", 256, 512), A("Iq"), A(rw, 0, 256))])
-            act(A("nr"), A("M", 0, 256), ID)
-            act(A("OVP"), A("M", 256, 512), ID)
-            dma("Y", T.yvp[:], (T.OVP[0:128:16, :], "OVP", 0, 256, 256), 8192)
+        if t < NV - 1:
+            ts(A(lo, 16, 32), A("ui", 48, 64), 2.0, OP.mult)
+            act(A(lo, 0, 16), A(ls, 16, 32), IDN, bias=-1.0)
+            send(A("ls%d" % (t + 1)), A(lo))
+            tt(LH1(t, 0), A("ui", 32, 48), A("Jn"), OP.add)
+            ts(A("on"), LH1(t, 0), 2048.0, OP.add)
         else:
-            torows([(A("M"), A("Id"), A("Jz"))])
-            act(A("rf", 0, 256), A("M", 256, 512), ID)
-            narrow(A(vr), A("rf", 0, 256))
-            act(A("nr"), A("M", 0, 256), ID, bias=4096.0)
-            act(A(lo, 16, 32), A(ls, 0, 16), ID, bias=-0.5)
-            send([(A("rw%d" % (t + 1), 0, 256), A(vr)), (A("rw%d" % (t + 1), 256, 512), A(rw, 0, 256))], 4)
-        for o in ops[n0:]:
-            o["b"] = BU
-        if UFIRST:
-            edits()
-        if not last:
-            send([(A("ls%d" % (t + 1)), A(lo))], 4)
-
-        def look2(c):
-            a, b = CH * c, CH * c + CH
-            win = IND(A("W", 0, 6145), A("o2", a, b))
-            if c in L2S:
-                gl, fam = "GF%d" % (ngf[0] % 3), "F1f"
-                ngf[0] += 1
-                act(A(gl), win, ID, bias=-6143.0)
-                if c in L2G:
-                    for h in range(2):
-                        narrow(A("GH" + gl[2], 512 * h, 512 * h + 512), A(gl, 512 * h, 512 * h + 512))
-                    gl, fam = "GH" + gl[2], "F1"
-            else:
-                gl, fam = "GL%d" % (ngl[0] % 3), "F1"
-                ngl[0] += 1
-                ts(A(gl), win, -6143.0, OP.add)
-            e = B2[c]
-            st = 4 if fam == "F1f" else 16
-            for k0 in range(0, 16, st):
-                mm([(A(e, 0, CH), F(fam, k), A(gl, k, 16 * CH, 16), k == 0, k == 15) for k in range(k0, k0 + st)])
-            ts(A("o3", a, b), A(e, 0, CH), 2048.0, OP.add)
-
-        def look3(c):
-            a, b = CH * c, CH * c + CH
-            gl = "GL%d" % (ngl[0] % 3)
-            ngl[0] += 1
-            ts(A(gl), IND(A("W", 0, 6145), A("o3", a, b)), -6144.0, OP.add, 0.5, OP.mult)
-            e = B3[c]
-            grp([(A(e, 0, CH), A("I3"), A("oneb", 0, CH))] + [(A(e, 0, CH), F("F1", k), A(gl, k, 16 * CH, 16)) for k in range(16)])
-            ts(A("mm", a, b), A(e, 0, CH), 4096.0, OP.is_lt, 1.0, OP.add)
-            tt(A("PV", a, b), A(e, 0, CH), A("mm", a, b), OP.mult)
-            ts(A("o4", a, b), A("PV", a, b), -4096.0, OP.add)
-
-        def lines(c):
-            a, b = CH * c, CH * c + CH
-            m = a + XV[c]
-            if m > a:
-                cp(A("G", 16 * a, 16 * m), IND(A("X"), A("o4", a, m)))
-            if m < b:
-                act(A("G", 16 * m, 16 * b), IND(A("X"), A("o4", m, b)), ID)
+            LQ = lambda a: (T.lq[:, a, :], "lq", 16 * a, 16 * a + 16, 16)
+            tt(LQ(0), A("ui", 32, 48), A("Jn"), OP.add)
+            ts(LQ(1), A(ls, 0, 16), 0.5, OP.mult, -0.5, OP.add)
+            ts(LQ(2), A(ls, 16, 32), 0.5, OP.mult, -1.0, OP.add)
             for h in range(2):
-                d = "D%d" % h
-                lst = []
-                for kk in range(8):
-                    o = A(d, CH * kk, CH * kk + CH)
-                    lst += [(o, A("Id"), A("G", 16 * a + 8 * h + kk, 16 * b, 16), True, False), (o, A("In"), A(zz, a, b), False, True)]
-                mm(lst)
-                act(A("Ab", 16 * a + 512 * h, 16 * a + 512 * h + 512), A(d), ABS)
-            kb = "K%d" % ([n for n, r in enumerate(TAIL) if r[0] <= a < r[1]][0] % 2)
-            for h in range(2):
-                mm([(A(kb, a, b), A("Ik"), A("oneb", 0, CH), True, False)] * (1 - h) +
-                   [(A(kb, a, b), Z("Z16", k), A("Ab", 16 * a + CH * k, 16 * a + CH * k + CH), False, k == 15) for k in range(8 * h, 8 * h + 8)])
+                ts(A("on", 8 * h, 8 * h + 8), (T.lq[:, 0, 8 * h:8 * h + 8], "lq", 0, 16, 8), 2048.0 * (1 - h), OP.add)
+            cp(A("lv"), A("ui", 48, 64))
+            grp([(A("M", 0, 256), A("Iq"), A("rw3", 256, 512))] + [(A("M", s, 256, 16), F("F3", s), A("lv")) for s in range(16)])
+            act(A("OVP"), A("M", 0, 256), IDN)
+            dma("Y", T.yvp[:], (T.OVP[0:128:16, :], "OVP", 0, 256, 256), 8192)
 
-        def tail(n):
-            a, b = TAIL[n]
-            kb, e = "K%d" % (n % 2), "E%d" % (n % 2)
-            if last:
-                ts(A("PV", a, b), A("PV", a, b), -4096.0, OP.add)
-            tt(A("PV", 256 + a, 256 + b), A("nr", a, b), A("PV", a, b), OP.subtract)
-            tr(A("kU", a, b), A(kb, a, b))
-            act(A("sg", a, b), A(kb, a, b), SIGN, bias=thr, scale=-1.0, acc=None if last else A("acc", n, n + 1))
-            o, d0, d1 = A("sc", a, b), A("d0", a, b), A("kU", a, b)
-            add("V", lambda: V.tensor_tensor_scan(o[0], d0[0], d1[0], 0.0, OP.add, OP.min), [o], [d0, d1], FIX + CY * (b - a))
-            tt(A("ohU", a, b), IND(A("sc", a, b), A("oc", 0, (b - a) // 16)), A("kU", a, b), OP.is_equal)
-            tr(A("oh", a, b), A("ohU", a, b))
-            wq = A("Id") if last else A("I2")
-            mm([(A(e, a, b), wq, A(rw, 256 + a, 256 + b), True, False), (A(e, a, b), A("Im"), A("sg", a, b), False, True),
-                (A(e, 256 + a, 256 + b), wq, A(rw, a, b), True, False), (A(e, 256 + a, 256 + b), A("Ip"), A("sg", a, b), False, True)])
-            act(A("Q", a, b), A(e, a, b), ID, bias=-4096.0 if last else 0.0)
-            act(A("Q", 256 + a, 256 + b), A(e, 256 + a, 256 + b), ID, bias=-4096.0 if last else 1.0)
-            tt(A("t1", a, b), A("oh", a, b), A("PV", 256 + a, 256 + b), OP.mult)
-            tt(A("ee", a, b), A("t1", a, b), A("PV", a, b), OP.add)
-            wv, wp = (A("OV"), A("OPD")) if last else (A("W", 4096, WW), A("W", 4096, WW))
-            tt(IND(wv, A("os", a // 16, b // 16)), A("ee", a, b), A("Q", a, b), OP.max)
-            tt(IND(wp, A("os", 16 + a // 16, 16 + b // 16)), A("ee", a, b), A("Q", 256 + a, 256 + b), OP.max)
+    def threshold(t):
+        if t == 0:
+            return -0.5
+        grp([(A("M", 0, 1), A("onef"), A("acc", h, h + 1)) for h in range(2)])
+        ts(A("ai", 0, 1), A("M", 0, 1), -0.5, OP.mult, 16384.0, OP.add)
+        ts(A("ai", 1, 2), A("ai", 0, 1), 255, OP.bitwise_and)
+        ts(A("thr"), A("ai", 1, 2), 16.0, OP.mult, -0.5, OP.add)
+        return A("thr")
 
-        def nearest(a, b, bl, bx):
-            ca, cb = a // 16, b // 16
-            grp([(A(bl, ca, cb), A("Id"), A("Jh", ca, cb))] + [(A(bl, ca, cb), Z("Zk", s), A("oh", a + s, b, 16)) for s in range(16)])
-            cp(A("ox", ca, cb), A(bl, ca, cb))
-            act(A("xs", a, b), IND(A("G", 16 * a, 16 * b), A("ox", ca, cb)), ID)
-            mm([(A(bx, a, b), A("Id"), A("xs", a, b), True, False), (A(bx, a, b), A("Id"), A(zz, a, b), False, True),
-                (A(bx, 256 + a, 256 + b), A("Id"), A("xs", a, b), True, False), (A(bx, 256 + a, 256 + b), A("In"), A(zz, a, b), False, True)])
-            if not last:
-                act(A(zn, a, b), A(bx, 256 + a, 256 + b), ABS)
-            act(A("xr", a, b), A(bx, a, b), ID, bias=127.75, scale=0.5)
-            tt(IND(A("X", 16 * a, 16 * b), A("on", ca, cb)), A("xr", a, b), A("m128", a, b), OP.add)
-            if last:
-                act(A(zn, a, b), A(bx, 256 + a, 256 + b), ABS)
+    def directories():
+        for out, win, bias in (("OV", VDw, 2048.0), ("OPD", PDw, 2047.5)):
+            for a in (0, 512):
+                act(A("M"), win(a, a + 512), IDN, scale=0.5, bias=bias)
+                tt(A(out, a, a + 512), win(a, a + 512), A("M"), OP.min)
 
-        for w in SEQ.split():
-            (look2 if w[0] == "2" else look3)(int(w[1]))
-        for c in range(NCH):
-            lines(c)
-            for n, r in enumerate(TAIL):
-                if r[1] == CH * c + CH:
-                    tail(n)
+    def packed(hh, qs):
+        mm([(A("E%d" % hh), A(("Id", "Ia", "I4", "Ic")[q]), A("X", 1024 * q + 512 * hh, 1024 * q + 512 * hh + 512), q == 0, q == 3) for q in qs])
+
+    for t in range(NV):
+        last = t == NV - 1
+
+
+        def do(name, fn, *args):
+            at(t, name)
+            return fn(*args)
+
+        thr = do("thr", threshold, t)
+        if t == 0:
+            look1(0)
+            for c in range(4):
+                do("f%d" % c, look2, 0, L2_FIRST[c])
+                if c:
+                    do("l3%d" % (c - 1), look3, 0, c - 1)
+            do("rows0", rows, 0)
+            repeats(0, 0, 0, "ls0")
+            do("ed0", edits, 0)
+            do("on", onward, 0)
+            do("g0", lines, 0, 0)
+            do("l33", look3, 0, 3)
+        else:
+            do("l30", look3, t, 0)
+            do("l31", look3, t, 1)
+            for u in L2_LATER[AHEAD:]:
+                do("l22", look2, t, u)
+            do("l32", look3, t, 2)
+            do("g0", lines, t, 0)
+            do("l33", look3, t, 3)
+            do("pd1", entries, t - 1, 1, 0)
+            do("on", onward, t)
+        do("e0", early, t, 0)
+        do("g1", lines, t, 1)
+        if last:
+            do("dir", directories)
+        do("t0", tail, t, 0, thr)
+        do("n0", nearest, t, 0)
+        do("g2", lines, t, 2)
+        do("e1", early, t, 1)
+        do("g3", lines, t, 3)
+        do("x0", newline, t, 0)
+        if last:
+            packed(0, (0, 1))
+            packed(1, (0, 1))
+        else:
+            do("ptr", pointers, t)
+            do("l1", look1, t + 1)
+            do("rows", rows, t + 1)
+            do("l20", look2, t + 1, L2_LATER[0])
+            for u in L2_LATER[1:AHEAD]:
+                do("l21", look2, t + 1, u)
+            do("ed", edits, t + 1)
+        do("t1", tail, t, 1, thr)
         if last:
             dma("Y", T.yvd[:], A("OV", 0, 1024), 524288)
-            dma("S", T.ypd[:], A("OPD", 0, 1024), 1000000)
-            yx = lambda h, qs: mm([(A("D%d" % h), A(("Id", "Ia", "Ib", "Ic")[q]), A("X", 1024 * q + 512 * h, 1024 * q + 512 * h + 512),
-                                    q == 0, q == 3) for q in qs])
-            nearest(0, 192, "M", "M")
-            yx(0, (0, 1, 2))
-            yx(1, (0, 1, 2))
-            nearest(192, 256, "K1", "K1")
-            dma("Y", T.yz[:], A(zn), 65536)
-            for h in range(2):
-                yx(h, (3,))
-                if h == 0:
-                    act(A("OX", 0, 512), A("D0"), ID)
-                else:
-                    cp(A("OX", 512, 1024), A("D1"))
-                dma("S" if h == 0 else "Y", T.yx[:, 512 * h:512 * h + 512], A("OX", 512 * h, 512 * h + 512), 600000)
-        else:
-            for (a, b), bk in zip(((0, 192), (192, 256)), NB):
-                n0 = len(ops)
-                nearest(a, b, bk[0], bk[1])
-                send([(A("zz%d" % (t + 1), a, b), A(zn, a, b))], 4)
-                for o in ops[n0:n0 + 5] + ops[-1:]:
-                    o["b"] = BZ
-            if EARLY:
-                dups(("rw%d" % (t + 1), 0), ("ls%d" % (t + 1), 0), "lo%d" % (t + 1))
+            dma("Y", T.ypd[:], A("OPD", 0, 1024), 1000000)
+        do("n1", nearest, t, 1)
+        do("x1", newline, t, 1)
+        if last:
+            dma("Y", T.yz[:], A("zn3"), 65536)
+            for hh in range(2):
+                packed(hh, (2, 3))
+            act(A("OX", 0, 512), A("E0"), IDN)
+            cp(A("OX", 512, 1024), A("E1"))
+            dma("S", T.yx[:, 0:512], A("OX", 0, 512), 400000)
+            dma("Y", T.yx[:, 512:1024], A("OX", 512, 1024), 600000)
     return ops
 
 
@@ -508,7 +541,7 @@ def depend(ops):
 
 
 def key(o):
-    nm = lambda a: (a[0][:2] if a[0][:2] in ("zn", "zz", "lo", "ls", "rw", "vr", "GL", "GF", "GH") else a[0]) + str(a[1])
+    nm = lambda a: (a[0][:2] if a[0][:2] in ("zn", "zz", "lo", "ls", "lh", "rw", "os", "GL", "GF") else a[0]) + str(a[1])
     return o["e"] + "".join(nm(a) for a in o["w"][:1] + o["r"][-1:])
 
 
@@ -561,7 +594,7 @@ def search(g, T, core, topo):
         return st
 
     def topo_order(pr, edges, back):
-        left, heap, seq = [len(e) for e in edges], [], []
+        left, seq = [len(e) for e in edges], []
         heap = sorted((pr[i], i) for i in range(n) if left[i] == 0)
         while heap:
             i = heap.pop(0)[1]
@@ -577,15 +610,24 @@ def search(g, T, core, topo):
         return seq
 
     zero = [0.0] * n
+    far = [0.0] * n
+    for i in range(n - 1, -1, -1):
+        far[i] = ops[i]["d"] + max([w + far[j] for j, w in post[i]] + [tail[i]])
+    due = [o["at"] for o in ops]
+    for i in range(n - 1, -1, -1):
+        due[i] = min([due[i]] + [due[j] - w - ops[i]["d"] for j, w in post[i]])
+    st = place(topo_order([due[i] - ops[i].get("b", 0.0) for i in range(n)], pre, post), pre, zero)
+    if ROUNDS < 0:
+        order = sorted(range(n), key=lambda i: (st[i], i))
+        return order, [replay(o, order, deps, c) for o, c in zip(vs, COSTS)], st
     x, best, top = 12345, None, None
-    st = schedule(ops, deps, {})[2]
     for r in range(ROUNDS + 1):
         move = {}
         for m in range(r % 5 if r else 0):
             x = (x * 1103515245 + 12345) % 2147483648
             k = names[(x >> 8) % len(names)]
             x = (x * 1103515245 + 12345) % 2147483648
-            move[k] = (-6, -3, -2, -1, 1, 2, 3, 6)[(x >> 8) % 8] * 500.0
+            move[k] = (-6, -3, -2, -1, 1, 2, 3, 6)[(x >> 8) % 8] * 400.0
         base = best[2] if best else st
         if r % 2 == 0:
             bk = place(topo_order([-base[i] - ops[i]["d"] - move.get(keys[i], 0.0) for i in range(n)], post, pre), post, tail)
@@ -602,49 +644,128 @@ def search(g, T, core, topo):
     return top[1], top[0], top[2]
 
 
-def schedule(ops, deps, TUNE):
+def anneal(vs, deps, costs, order, rounds, heat, seed=12345):
+    ops = vs[0]
     n = len(ops)
-    HOP = COSTS[0][5]
-    lat = [o["x"][2] if o["k"] != "c" else HOP for o in ops]
-    succ = [[] for _ in ops]
+    reach, few = [], []
+    for i in range(n):
+        r = 0
+        for j in deps[i]:
+            r |= reach[j]
+        few.append({j for j in deps[i] if not r >> j & 1 or ops[j]["k"] != "c"})
+        for j in deps[i]:
+            r |= 1 << j
+        reach.append(r)
+    deps = few
+    lag = lambda o, C, j, i: o[j]["x"][2] if o[j]["k"] != "c" else C[5] if o[j]["e"] != o[i]["e"] else 0.0 if o[j]["e"] == "P" else C[6]
+    pre = [[[(j, o[j]["d"] + lag(o, C, j, i)) for j in deps[i]] for i in range(n)] for o, C in zip(vs, costs)]
+    dur = [[x["d"] for x in o] for o in vs]
+    end = [[x["d"] + (x["x"][2] if x["k"] != "c" else 0.0) for x in o] for o in vs]
+    post = [[] for _ in ops]
     for i in range(n):
         for j in deps[i]:
-            succ[j].append(i)
-    pr = [0.0] * n
-    nxt = {}
-    for i in range(n - 1, -1, -1):
-        pr[i] = ops[i]["d"] + lat[i] + max([pr[s] for s in succ[i]] + [0.0])
-        tag = (ops[i]["e"], CHAIN.get(ops[i]["w"][0][0] if ops[i]["w"] else ""))
-        if tag[1]:
-            pr[i] = max(pr[i], ops[i]["d"] + nxt.get(tag, 0.0))
-            nxt[tag] = pr[i]
-    for i in range(n):
-        pr[i] += ops[i].get("b", 0.0) + TUNE.get(key(ops[i]), 0.0)
-    left = [len(d) for d in deps]
-    rdy = [0.0] * n
-    free = {e: 0.0 for e in ENG}
-    cand = [i for i in range(n) if left[i] == 0]
-    order, start = [], [0.0] * n
-    while cand:
-        t0 = min(max(rdy[i], free[ops[i]["e"]]) for i in cand)
-        e = [ops[i]["e"] for i in cand if max(rdy[i], free[ops[i]["e"]]) == t0][0]
-        mine = [i for i in cand if ops[i]["e"] == e]
-        now = [i for i in mine if rdy[i] <= t0 + 60]
-        i = max(now, key=lambda x: (pr[x], -x))
-        soon = [x for x in mine if rdy[x] < t0 + 0.5 * ops[i]["d"] and pr[x] > pr[i] + ops[i]["d"]]
-        if soon:
-            i = min(soon, key=lambda x: (rdy[x], -pr[x]))
-        cand.remove(i)
-        start[i] = max(rdy[i], free[e])
-        free[e] = start[i] + ops[i]["d"]
-        order.append(i)
-        for s in succ[i]:
-            same = ops[s]["e"] == e and ops[i]["k"] == "c"
-            rdy[s] = max(rdy[s], free[e] + ((0 if e == "P" else 40) if same else lat[i]))
-            left[s] -= 1
-            if left[s] == 0:
-                cand.append(s)
-    return order, deps, start
+            post[j].append(i)
+    need = [len(d) for d in deps]
+
+    def run(seq):
+        before, after = [-1] * n, [-1] * n
+        left = list(need)
+        for q in seq.values():
+            for a, b in zip(q, q[1:]):
+                before[b], after[a] = a, b
+                left[b] += 1
+        todo = [i for i in range(n) if left[i] == 0]
+        for i in todo:
+            for k in post[i]:
+                left[k] -= 1
+                if left[k] == 0:
+                    todo.append(k)
+            k = after[i]
+            if k >= 0:
+                left[k] -= 1
+                if left[k] == 0:
+                    todo.append(k)
+        if len(todo) < n:
+            return None
+        sts, ts = [], []
+        for p, d, e in zip(pre, dur, end):
+            st = [0.0] * n
+            for i in todo:
+                k = before[i]
+                s = st[k] + d[k] if k >= 0 else 0.0
+                for j, w in p[i]:
+                    w += st[j]
+                    if w > s:
+                        s = w
+                st[i] = s
+            sts.append(st)
+            ts.append(max([a + b for a, b in zip(st, e)]))
+        return ts, sts, before, todo
+
+    def chain(res, m):
+        ts, sts, before, todo = res
+        st, out = sts[m], []
+        i = max(range(n), key=lambda k: st[k] + end[m][k])
+        while st[i] > 0:
+            k = before[i]
+            if k >= 0 and st[k] + dur[m][k] >= st[i] - 1e-6:
+                if k not in deps[i] and ops[i]["e"] != "Y":
+                    out.append((k, i))
+                i = k
+            else:
+                i = max(pre[m][i], key=lambda x: st[x[0]] + x[1])[0]
+        return out
+
+    seq = {e: [i for i in order if ops[i]["e"] == e] for e in ENG}
+    seq["Y"].sort()
+    cur = run(seq)
+    top, x = (cur, seq), seed
+    chains = {}
+    for r in range(rounds):
+        x = (x * 1103515245 + 12345) % 2147483648
+        m = (x >> 8) % len(vs)
+        if m not in chains:
+            chains[m] = chain(cur, m)
+        if not chains[m]:
+            continue
+        x = (x * 1103515245 + 12345) % 2147483648
+        a, b = chains[m][(x >> 8) % len(chains[m])]
+        x = (x * 1103515245 + 12345) % 2147483648
+        far, back = (0, 0, 1, 2, 4, 8, 16)[(x >> 8) % 7], (x >> 20) % 2
+        e = ops[a]["e"]
+        q = list(seq[e])
+        p = q.index(a)
+        if back:
+            k = p
+            while k > 0 and p - k < far and q[k - 1] not in deps[b]:
+                k -= 1
+            q.pop(p + 1)
+            q.insert(k, b)
+        else:
+            k = p + 1
+            while k + 1 < len(q) and k - p - 1 < far and a not in deps[q[k + 1]]:
+                k += 1
+            q.pop(p)
+            q.insert(k, a)
+        new = dict(seq)
+        new[e] = q
+        res = run(new)
+        if res is None:
+            continue
+        x = (x * 1103515245 + 12345) % 2147483648
+        if sum(res[0]) <= sum(cur[0]) + len(vs) * heat * (1.0 - r / rounds) * ((x >> 8) % 1000 / 1000.0) ** 2:
+            cur, seq, chains = res, new, {}
+            if sum(cur[0]) < sum(top[0][0]):
+                top = (cur, seq)
+    st = top[0][1][0]
+    rank = {i: k for k, i in enumerate(top[0][3])}
+    return sorted(range(n), key=lambda i: (st[i], rank[i])), top[0][0], st
+
+
+def plan(g, T, core, topo):
+    costs = [COSTS[k] for k in ANNEAL[0]]
+    vs = [build(g, T, core, topo, C) for C in costs]
+    return anneal(vs, depend(vs[0]), costs, search(g, T, core, topo)[0], ANNEAL[1], ANNEAL[2])
 
 
 def emit(g, T, ops, order, deps):
@@ -705,6 +826,6 @@ def rank_program(g, core, T, topo):
     if T.rank_of(core) is None:
         return
     if not PLAN:
-        PLAN.append(search(g, T, core, topo)[0])
+        PLAN.append(plan(g, T, core, topo)[0])
     ops = build(g, T, core, topo, COSTS[0])
     emit(g, T, ops, PLAN[0], depend(ops))

from concourse.bass import DstId, RemoteDMATransfer
from concourse.mybir import AluOpType as OP, ActivationFunctionType as AF

NV = 4
ID = 256
DIR, PP = ID + 4096, 6664
WW = ID + PP + 128
L2_FIRST = ((("V", 0, 64),), (("S", 64, 128),), (("S", 128, 192),), (("S", 192, 256),))
L2_LATER = ((("V", 0, 64),), (("S", 64, 96), ("S", 96, 128)), (("S", 128, 160), ("S", 160, 192)), (("S", 192, 224), ("S", 224, 256)))
AHEAD = 3
PIECE = 32
L3V = ((64, 64, 64, 64), (64, 64, 64, 64), (64, 64, 64, 64), (64, 64, 64, 64))
XV = ((0, 0, 0, 0), (0, 0, 0, 0), (0, 0, 0, 0), (0, 0, 0, 0))
START, PERIOD = 10.0, 21.0
WHEN = {"thr": 3.0, "l30": 0.0, "l31": 2.7, "l32": 5.3, "l33": 7.4, "l22": 0.3, "pd1": 4.5, "on": 3.5, "g0": 2.9, "g1": 5.5, "g2": 8.5,
        "g3": 10.5, "e0": 6.0, "t0": 8.5, "n0": 9.8, "e1": 12.0, "x0": 14.5, "ptr": 11.5, "l1": 12.5, "rows": 10.0, "l20": 13.5,
        "l21": 18.0, "ed": 15.0, "t1": 17.5, "n1": 18.8, "x1": 22.6, "dir": 6.0, "top": 4.0, "out": 20.0}
WHEN0 = {"f0": -2.0, "f1": -2.0, "f2": -0.5, "f3": 1.0, "rows0": 1.0, "ed0": 4.0}
PLAN = []
f32, bf, f16, i32, u16 = "float32", "bfloat16", "float16", "int32", "uint16"


def _sb(n, d):
    return ("sbuf", [128] + (n if isinstance(n, list) else [n]), d)


SCRATCH = {
    "W": _sb(WW, f32), "X": _sb(4096, bf), "G": _sb(4096, bf), "Ab": _sb([16, 256], bf),
    "rv": _sb(1024, i32), "rp": _sb(1024, i32), "pv": _sb(32, i32), "wti": _sb(1, i32), "thi": _sb(1, i32),
    "GL0": _sb(1024, f16), "GL1": _sb(1024, f16), "GL2": _sb(1024, f16), "GH": _sb(4096, f16),
    "GF0": _sb(1024, f32), "GF1": _sb(1024, f32), "GF2": _sb(1024, f32), "GF3": _sb(1024, f32),
    "o1": _sb(16, u16), "o2": _sb(256, u16), "o3": _sb(256, u16), "o4": _sb(256, u16),
    "on": _sb(16, u16), "ox": _sb(16, u16), "oc": _sb(8, u16), "of": _sb(2, u16),
    "F1": _sb(2048, bf), "F3": _sb(2048, bf), "mk": _sb(16, f32), "Zw": _sb(144, bf), "Zn": _sb(144, bf),
    "Bk": _sb(128, bf), "Tri": _sb(128, bf), "Bi": _sb(128, f32), "sel": _sb(16, bf), "KC": _sb(256, f16), "TC": _sb(512, bf),
    "oneb": _sb(512, bf), "onef": _sb(128, f32), "m128": _sb(128, bf), "d0": _sb(128, f32),
    "jl": _sb(16, f32), "Jn": _sb(16, f32), "Jh": _sb(8, f16), "J": _sb(32, f32), "mo": _sb(256, f32),
    "pi": _sb(1, i32), "ci": _sb(4, i32), "cf": _sb(8, f32),
    "E": _sb([16, 256], bf), "dsg": _sb(256, bf), "rf": _sb(512, f32),
    "sc": _sb(256, f32), "ky": _sb(256, f32), "oh": _sb(256, bf), "sg": _sb(256, bf), "es": _sb(256, f32), "rr": _sb(128, f32),
    "eqN": _sb(256, bf), "xs": _sb(256, bf), "xr": _sb(256, bf), "ee": _sb(128, f32), "tov": _sb(256, f32), "top": _sb(256, f32),
    "acc": _sb(2, f32), "thr": _sb(1, f32), "ai": _sb(2, i32), "ui": _sb(64, i32), "uf": _sb(32, f32), "lv": _sb(16, f16),
    "dl": _sb(96, f32), "lq": _sb([3, 16], f16),
    "OV": _sb(1280, f32), "OPD": _sb(1280, f32), "OX": _sb(1024, f32), "OVP": _sb(256, f32),
}
SCALED = (("Id", 1.0), ("In", -1.0), ("I3", 3072.0), ("I4", 4096.0), ("Im4", -4096.0), ("Ia", 64.0), ("Ic", 262144.0), ("Iq", 512.0))
for _n, _c in SCALED:
    SCRATCH[_n] = _sb(128, bf)
for _t in range(NV):
    SCRATCH["zz%d" % _t] = _sb(256, bf)
    SCRATCH["zn%d" % _t] = _sb(256, bf)
    SCRATCH["ls%d" % _t] = _sb(64, f32)
    SCRATCH["lo%d" % _t] = _sb(64, f32)
    SCRATCH["lh%d" % _t] = _sb([3, 16], f16)
    SCRATCH["rw%d" % _t] = _sb(512, f16)
    SCRATCH["os%d" % _t] = _sb(32, u16)
PS = ["D0", "D1", "E0", "E1", "K", "T", "N", "M"]
for _n in PS:
    SCRATCH[_n] = ("psum", [128, 512], f32)
ENG = "VSPGY"
NDMA = 24
SEMAPHORES = ["eV", "eS", "eP", "eG", "sent"] + ["d%d" % i for i in range(NDMA)] + ["a%d" % i for i in range(9)]

COSTS = [(0.92, 0.46, 40.0, 1.56, 3.8, 120.0, 50.0, 3000.0), (0.92, 0.46, 40.0, 1.1, 2.0, 120.0, 50.0, 3000.0),
         (0.92, 0.46, 40.0, 2.0, 5.5, 120.0, 50.0, 3000.0), (1.15, 0.58, 40.0, 1.56, 3.8, 120.0, 50.0, 2500.0),
         (0.92, 0.46, 60.0, 1.56, 3.8, 250.0, 100.0, 4500.0)]
ROUNDS, SLACK = 100, 1500.0
ANNEAL = ((0, 4), 80000, 1500.0)


def build(g, T, core, topo, C):
    CY, PCY, FIX, GA, SCA = C[:5]
    ops = []
    rank = T.rank_of(core)
    nxt = T.cores[(rank + 1) % len(T.cores)]
    rid, pid, _ = topo.addr(nxt)
    engs = topo.engines(core, nxt)
    V, S, P = g.vector, g.scalar, g.tensor
    nd, na, now = [0], [0], [0.0]

    def A(name, lo=None, hi=None, step=None):
        t = T[name]
        if lo is None:
            return (t[:], name, 0, t.shape[1], t.shape[1])
        if step is None:
            return (t[:, lo:hi], name, lo, hi, hi - lo)
        return (t[:, lo:hi:step], name, lo, hi, len(range(lo, hi, step)))

    def IND(win, off):
        return (win[0].indirect(off[0]), win[1], win[2], win[3], 16 * off[4], off)

    def add(eng, fn, outs, ins, dur, kind="c", extra=None):
        rd, wr = [], []
        for a in ins:
            if isinstance(a, tuple):
                rd.append(a[1:4])
                if len(a) > 5:
                    rd.append(a[5][1:4])
        for a in outs:
            wr.append(a[1:4])
            if len(a) > 5:
                rd.append(a[5][1:4])
        ops.append({"e": eng, "fn": fn, "r": rd, "w": wr, "d": dur, "k": kind, "x": extra, "at": now[0]})
        now[0] += dur + 100.0

    def at(t, name):
        now[0] = 1000.0 * (START + PERIOD * t + (WHEN0 if t == 0 and name in WHEN0 else WHEN)[name])

    def ap(a):
        return a[0] if isinstance(a, tuple) else a

    def two(a):
        return SCRATCH[a[1]][2] in (bf, f16, u16)

    def vd(o, i, rate):
        if len(o) > 5:
            return 50 + SCA * CY * o[4]
        if len(i) > 5:
            return 50 + GA * CY * i[4]
        return FIX + CY * max(48, rate * o[4])

    def cp(o, i):
        add("V", lambda: V.tensor_copy(o[0], i[0]), [o], [i], vd(o, i, 0.5 if two(o) and two(i) else 1))

    def ts(o, i, s1, op0, s2=None, op1=None):
        if op1 is None:
            fn = lambda: V.tensor_scalar(o[0], i[0], ap(s1), None, op0)
        else:
            fn = lambda: V.tensor_scalar(o[0], i[0], ap(s1), ap(s2), op0, op1)
        add("V", fn, [o], [i, s1, s2], vd(o, i, 0.5 if two(o) and two(i) else 1))

    def tt(o, a, b, op):
        add("V", lambda: V.tensor_tensor(o[0], a[0], b[0], op), [o], [a, b], vd(o, a, 1 if (a[1] in PS or b[1] in PS) else 2))

    def ms(o, c):
        add("V", lambda: V.memset(o[0], c), [o], [], vd(o, o, 0.5 if two(o) else 1))

    def act(o, i, f, bias=0.0, scale=1.0, acc=None):
        if acc is None:
            fn = lambda: S.activation(o[0], i[0], f, bias=ap(bias), scale=ap(scale))
        else:
            fn = lambda: S.activation(o[0], i[0], f, bias=ap(bias), scale=ap(scale), accum_out=acc[0])
        add("S", fn, [o] + ([acc] if acc else []), [i, bias, scale],
            65 + GA * CY * i[4] if len(i) > 5 else FIX + CY * max(48, i[4]) + (20 if acc else 0))

    def mm(lst):
        def fn():
            r = None
            for o, l, x, st, sp in lst:
                r = P.matmul(o[0], l[0], x[0], st, sp)
            return r
        d = sum(max(64, x[4]) * (4 if SCRATCH[x[1]][2] == f32 else 1) * PCY + 3 for o, l, x, st, sp in lst)
        add("P", fn, [m[0] for m in lst], [m[1] for m in lst] + [m[2] for m in lst], d + 30)

    def grp(lst, start=True, stop=True):
        mm([(o, l, x, start and n == 0, stop and n == len(lst) - 1) for n, (o, l, x) in enumerate(lst)])

    def iota(o, pat, base, cm):
        if SCRATCH[o[1]][2] == i32:
            fn = lambda: g.iota(o[0], pat, base, cm)
        else:
            fn = lambda: g.iota(o[0], pat, base, cm, allow_small_or_imprecise_dtypes=True)
        add("G", fn, [o], [], 150 + 2 * CY * o[4])

    def select(o, i, pat, op, base, cm):
        add("G", lambda: g.affine_select(o[0], i[0], pat, op, 0.0, base, cm), [o], [i], 190 + 2 * CY * o[4])

    def gcopy(o, i):
        select(o, i, [[0, o[4]]], OP.is_ge, 0, 0)

    def dma(q, o, i, nbytes, slow=False):
        sem = T.sem["d%d" % nd[0]]
        nd[0] += 1
        Q = {"Y": g.sync, "S": g.scalar, "G": g}[q]
        if slow:
            fn = lambda: Q.dma_start(ap(o), ap(i), allow_slow_non_contiguous=True).then_inc(sem, 16)
        else:
            fn = lambda: Q.dma_start(ap(o), ap(i)).then_inc(sem, 16)
        add(q, fn, [o] if isinstance(o, tuple) else [], [i], 1000 if q == "G" else 80, "dma", (sem, 16, 1500 + nbytes / 250.0))

    def send(o, i):
        sem = T.sem["a%d" % na[0]]
        na[0] += 1
        m = 0
        for e in engs[:4]:
            m |= 1 << e
        add("G", lambda: g.remote_dma(o[0], i[0], sem, T.sem.sent, pid, rid, m), [o], [i], 800, "rem", (sem, 4, C[7]))

    IDN, ABS, SIGN = AF.Identity, AF.Abs, AF.Sign
    F = lambda n, k: A(n, 128 * k, 128 * k + 128)
    Z = lambda n, k: A(n, 15 - k, 143 - k)
    R = lambda a, b, st=None: A("W", ID + 1 + a, ID + 1 + b, st)
    VDw = lambda a, b: A("W", DIR + 2 + 2 * a, DIR + 1 + 2 * b, 2)
    PDw = lambda a, b: A("W", DIR + 1 + 2 * a, DIR + 2 * b, 2)
    col = lambda k: A("cf", k, k + 1)
    LH = lambda t, a, b: (T["lh%d" % t][:, a:b, :], "lh%d" % t, 16 * a, 16 * b, 16 * (b - a))
    LH1 = lambda t, a: (T["lh%d" % t][:, a, :], "lh%d" % t, 16 * a, 16 * a + 16, 16)

    dma("Y", A("rv", 0, 512), T.vdir[:, 0:512], 262144)
    dma("Y", A("rv", 512, 1024), T.vdir[:, 512:1024], 2 * 262144)
    dma("Y", A("pv", 16, 32), T.vn[:], 2 * 262144)
    dma("Y", A("rp", 0, 512), T.pdir[:, 0:512], 3 * 262144)
    dma("Y", A("rp", 512, 1024), T.pdir[:, 512:1024], 4 * 262144)
    dma("Y", A("pv", 0, 16), T.pn[:], 4 * 262144)
    dma("Y", A("zz0"), T.z[:], 4 * 262144)
    dma("Y", A("X"), T.xl[:], 8 * 262144)
    iota(R(0, 256), [[1, 256]], 0, 0)
    iota(A("pi"), [[0, 1]], 0, 1)
    for n, o in enumerate(ops):
        o["b"] = 1.0e6 * (20 - n)
    iota(R(3072, 4096), [[1, 1024]], 3072, 0)
    iota(A("Bi"), [[1, 8], [0, 16]], 0, 0)
    ms(A("oneb"), 1.0)
    ms(A("F1"), 0.0)
    ts(R(256, 512), R(0, 256), 256.0, OP.add)
    ts(R(512, 1024), R(0, 512), 512.0, OP.add)
    act(R(1024, 2048), R(0, 1024), IDN, bias=1024.0)
    ts(R(2048, 2560), R(0, 512), 2048.0, OP.add)
    act(R(2560, 3072), R(0, 512), IDN, bias=2560.0)
    cp(col(0), A("pi"))
    ts(A("ci", 0, 1), A("pi"), 15, OP.bitwise_and)
    ts(A("ci", 1, 2), A("pi"), 4, OP.arith_shift_right)
    cp(A("cf", 1, 3), A("ci", 0, 2))
    ts(A("Id"), R(0, 128), col(0), OP.is_equal)
    for n, c in SCALED[1:]:
        act(A(n), A("Id"), IDN, scale=c)
    ts(A("of", 0, 1), col(1), 128.0, OP.mult, col(0), OP.add)
    ts(A("mk"), R(0, 16), col(1), OP.is_equal)
    cp(IND(A("F1"), A("of", 0, 1)), A("mk"))
    for raw, win, bias, banks in (("rv", VDw, -4096.0, ("D0", "D1")), ("rp", PDw, -4095.0, ("T", "N"))):
        for h in range(2):
            a, b = 512 * h, 512 * h + 512
            ts(A(banks[h]), A(raw, a, b), 2.0, OP.mult, bias, OP.add)
            tt(win(a, b), A(raw, a, b), A(banks[h]), OP.max)
    ts(A("ls0", 16, 32), A("pv", 16, 32), 2.0, OP.mult)
    ts(A("ls0", 0, 16), A("pv", 0, 16), 2.0, OP.mult, -1.0, OP.add)
    now[0] = 1.0e6
    for q in range(4):
        select(A("F3", 512 * q, 512 * q + 512), A("oneb"), [[-1, 4], [-16, 8], [0, 16]], OP.is_equal, -4 * q, 1)
    dma("G", A("wti"), T.wt[:], 512, True)
    dma("G", A("thi"), T.th[:], 512, True)
    act(col(4), col(2), IDN, scale=16.0, bias=15.0)
    cp(col(5), A("wti"))
    ts(col(6), A("thi"), -16.0, OP.mult)
    ts(A("Zw"), R(0, 144), col(4), OP.is_equal, col(5), OP.mult)
    ts(A("Zn"), R(0, 144), col(4), OP.is_equal, col(1), OP.mult)
    for b in (0, 8):
        ts(A("sel", b, b + 8), R(0, 8), col(2), OP.is_equal, 16.0, OP.mult)
    ts(A("KC", 0, 128), A("Id"), col(1), OP.mult)
    ts(A("KC", 128, 256), A("Id"), col(6), OP.mult)
    iota(A("TC", 0, 256), [[2048, 2], [0, 128]], -4096, 0)
    gcopy(A("TC", 256, 512), A("oneb", 0, 256))
    ts(A("Bk"), A("Bi"), col(2), OP.is_equal)
    select(A("Tri"), A("Bk"), [[1, 128]], OP.is_gt, 0, -1)
    ms(A("onef"), 1.0)
    ms(A("m128"), -128.0)
    ms(A("d0"), 0.0)
    ms(A("d0", 0, 128, 16), 1.0e6)
    ts(A("jl"), R(0, 256, 16), col(1), OP.add)
    ts(A("oc"), R(0, 128, 16), 15.0, OP.add)
    ts(A("Jh"), A("jl", 0, 8), 16.0, OP.mult)
    act(A("Jn"), A("jl"), IDN, scale=16.0, bias=-2048.0)
    act(A("J", 0, 16), A("jl"), IDN, scale=2.0, bias=2047.0 - 4096.0)
    act(A("J", 16, 32), A("jl"), IDN, scale=2.0, bias=2048.0 - 4096.0)
    act(A("W", ID + PP, WW), R(0, 128), IDN, scale=2.0, bias=-1.0 - ID)
    ngl, ngf, ne = [0], [0], [0]

    def rows(t):
        cp(LH(t, 1, 3), A("ls%d" % t, 0, 32))
        lo = 0 if t == 0 else 256
        mm([(A("M", lo + s, 512, 16), F("F3", s), LH(t, 1, 3) if t == 0 else LH1(t, 2), True, True) for s in range(16)])
        act(A("rf", lo, 512), A("M", lo, 512), IDN)
        gcopy(A("rw%d" % t, lo, 512), A("rf", lo, 512))

    def repeats(t, r0, l0, out):
        for c in range(16):
            n = 256 - 16 * c
            ts((T.E[:, c, 0:n], "E", 256 * c, 256 * c + n, n), A("rw%d" % t, r0 + 16 * c, r0 + 256), A("ls%d" % t, l0 + c, l0 + c + 1), OP.is_equal)
        grp([(A("M", 0, 256), A("Tri"), (T.E[:, :, 0:16], "E", 0, 4096, 256))] +
            [(A("M", 16 * c + 16, 256), A("Bk"), (T.E[:, c, 16:256 - 16 * c], "E", 256 * c, 256 * c + 256, 240 - 16 * c)) for c in range(15)])
        act(A("dsg"), A("M", 0, 256), SIGN)
        grp([(A("M", 256, 272), F("F1", s), A("dsg", s, 256, 16)) for s in range(16)])
        for b in (32, 48):
            act(A(out, b, b + 16), A("M", 256, 272), IDN, scale=4096.0)

    def edits(t):
        ls, lo = "ls%d" % t, "lo%d" % t
        repeats(t, 256, 16, lo)
        tt(A("dl", 0, 32), A(lo, 32, 64), A(ls, 32, 64), OP.max)
        tt(A("dl", 32, 64), A("dl", 0, 32), A("J"), OP.add)
        tt(A("dl", 64, 96), A(ls, 0, 32), A("dl", 32, 64), OP.max)
        if t < NV - 1:
            ts(A("os%d" % t), A("dl", 64, 96), 2.0, OP.add)
        else:
            ts(A("os%d" % t), A("dl", 64, 96), 0.5, OP.mult, 0.25, OP.add)

    def entries(t, h, n):
        win = A("W", DIR, ID + PP) if t < NV - 1 else A(("OPD", "OV")[n])
        cp(IND(win, A("os%d" % t, 16 * n + 8 * h, 16 * n + 8 * h + 8)), A(("top", "tov")[n], 128 * h, 128 * h + 128))

    def pointers(t):
        win, os = A("W", DIR, ID + PP), "os%d" % t
        ts(IND(win, A(os, 24, 32)), R(0, 128), 1.0, OP.mult, PP - 1.0, OP.add)
        ts(IND(win, A(os, 8, 16)), R(0, 128), 2.0, OP.mult, -1.0 - ID, OP.add)

    def look1(t):
        ts(A("o1"), A("ls%d" % t, 16, 32), 2.0, OP.add)
        for a, b in ((0, 64), (64, 256)) if t == 0 else ((0, 256),):
            ts(A("o2", a, b), IND(A("W", DIR, DIR + 2056), A("o1", a // 16, b // 16)), 1.0, OP.add)

    def bank():
        ne[0] += 1
        return "E%d" % (ne[0] % 2)

    def look2(t, unit):
        for eng, a, b in unit:
            win = IND(A("W", ID, DIR + 2056 if t == 0 else WW), A("o2", a, b))
            if eng == "V":
                ts(A("GH", 16 * a, 16 * b), win, -2047.0, OP.add)
            else:
                gf = "GF%d" % (ngf[0] % 4)
                ngf[0] += 1
                act(A(gf, 0, 16 * (b - a)), win, IDN, bias=-2047.0)
                for c in range(0, 16 * (b - a), 512):
                    gcopy(A("GH", 16 * a + c, 16 * a + c + 512), A(gf, c, c + 512))
        a, b, e = unit[0][1], unit[-1][2], bank()
        grp([(A(e, 0, b - a), F("F1", k), A("GH", 16 * a + k, 16 * b, 16)) for k in range(16)])
        ts(A("o3", a, b), A(e, 0, b - a), 2048.0 + ID, OP.add)

    def look3(t, c):
        a, b, e, gl = 64 * c, 64 * c + 64, bank(), "GL%d" % (ngl[0] % 3)
        ngl[0] += 1
        m = a + L3V[t][c]
        if m > a:
            ts(A(gl, 0, 16 * (m - a)), IND(A("W", 0, DIR + 2056), A("o3", a, m)), -2048.0, OP.add, 0.5, OP.mult)
        for x in range(m, b, PIECE):
            gf = "GF%d" % (ngf[0] % 4)
            ngf[0] += 1
            act(A(gf, 0, 16 * PIECE), IND(A("W", 0, DIR + 2056), A("o3", x, x + PIECE)), IDN, scale=0.5, bias=-1024.0)
            for y in range(0, 16 * PIECE, 512):
                gcopy(A(gl, 16 * (x - a) + y, 16 * (x - a) + y + 512), A(gf, y, y + 512))
        grp([(A(e, 0, 64), A("I3"), A("oneb", 0, 64))] + [(A(e, 0, 64), F("F1", k), A(gl, k, 1024, 16)) for k in range(16)])
        ts(A("mo", a, b), A(e, 0, 64), 4096.0, OP.is_lt, 1.0, OP.add)
        tt(A("es", a, b), A(e, 0, 64), A("mo", a, b), OP.mult)
        ts(A("o4", a, b), A("es", a, b), -4096.0, OP.add)

    def lines(t, c):
        a, b, h = 64 * c, 64 * c + 64, c // 2
        m = a + XV[t][c]
        if m > a:
            cp(A("G", 16 * a, 16 * m), IND(A("X"), A("o4", a, m)))
        if m < b:
            act(A("G", 16 * m, 16 * b), IND(A("X"), A("o4", m, b)), IDN)
        if c % 2:
            grp([(A("K", 0, 256), A("oneb", 0, 128), A("KC"))], stop=False)
        for hh in range(2):
            d, lst = "D%d" % hh, []
            for kk in range(8):
                o = A(d, 64 * kk, 64 * kk + 64)
                lst += [(o, A("Id"), A("G", 16 * a + 8 * hh + kk, 16 * b, 16), True, False), (o, A("In"), A("zz%d" % t, a, b), False, True)]
            mm(lst)
            act((T.Ab[:, 8 * hh:8 * hh + 8, a:b], "Ab", 256 * hh + a, 256 * hh + b, 512), A(d), ABS)
            if c % 2:
                grp([(A("K", k, 256, 16), (T.Ab[:, k, 128 * h:128 * h + 128], "Ab", 256 * hh + 128 * h, 256 * hh + 128 * h + 128, 128), A("sel"))
                     for k in range(8 * hh, 8 * hh + 8)], start=False, stop=hh == 1)

    def early(t, h):
        n = "lh%d" % t if t < NV - 1 else "lq"
        lh = (T[n][:, :, 8 * h:8 * h + 8], n, 0, 48, 24)
        grp([(A("T"), A("Id"), A("TC"))] + [(A("T", 128 + s, 512, 16), F("F3", s), lh) for s in range(16)], stop=False)

    def tail(t, h, thr):
        a, b, last = 128 * h, 128 * h + 128, t == NV - 1
        o, d0, d1 = A("sc", a, b), A("d0"), A("ky", a, b)
        act(d1, A("K", 0, 128), IDN)
        add("V", lambda: V.tensor_tensor_scan(o[0], d0[0], d1[0], 0.0, OP.add, OP.min), [o], [d0, d1], FIX + CY * 128)
        act(A("sg", a, b), A("K", 128, 256), SIGN, bias=thr, scale=-1.0, acc=None if last else A("acc", h, h + 1))
        tt(A("oh", a, b), IND(A("sc", a, b), A("oc")), d1, OP.is_equal)
        grp([(A("T", 256, 384), A("sg", a, b), A("Im4")), (A("T", 384, 512), A("sg", a, b), A("I4"))], start=False, stop=False)
        grp([(A("T", 0, 128), A("oh", a, b), A("Im4")), (A("T", 128, 256), A("oh", a, b), A("I4"))], start=False)
        grp([(A("N", 0, 128), A("oh", a, b), A("Id"))])
        act(A("eqN", a, b), A("N", 0, 128), IDN)
        ee = A("W", 0, ID, 2) if h and not last else A("ee")
        tt(A("rr"), A("es", a, b), A("T", 0, 128), OP.add)
        tt(ee, A("rr"), A("T", 128, 256), OP.max)
        tt(A("tov", a, b), ee, A("T", 256, 384), OP.max)
        entries(t, h, 1)
        tt(A("top", a, b), ee, A("T", 384, 512), OP.max)
        if last or not h:
            entries(t, h, 0)

    def nearest(t, h):
        a, b, zz, zn = 128 * h, 128 * h + 128, "zz%d" % t, "zn%d" % t
        grp([(A("N", 256, 264), A("Id"), A("Jh"))] + [(A("N", 256, 264), Z("Zn", s), A("eqN", a + s, b, 16)) for s in range(16)])
        cp(A("ox", 8 * h, 8 * h + 8), A("N", 256, 264))
        act(A("xs", a, b), IND(A("G", 16 * a, 16 * b), A("ox", 8 * h, 8 * h + 8)), IDN)
        mm([(A("N", 0, 128), A("Id"), A("xs", a, b), True, False), (A("N", 0, 128), A("In"), A(zz, a, b), False, True),
            (A("N", 128, 256), A("Id"), A("xs", a, b), True, False), (A("N", 128, 256), A("Id"), A(zz, a, b), False, True)])
        if t < NV - 1:
            act(A(zn, a, b), A("N", 0, 128), ABS)
            send(A("zz%d" % (t + 1), a, b), A(zn, a, b))
        act(A("xr", a, b), A("N", 128, 256), IDN, bias=127.75, scale=0.5)
        if t == NV - 1:
            act(A(zn, a, b), A("N", 0, 128), ABS)

    def newline(t, h):
        win = A("X", 2048 * h, 2048 * h + 2048) if t == NV - 1 else A("X")
        tt(IND(win, A("on", 8 * h, 8 * h + 8)), A("xr", 128 * h, 128 * h + 128), A("m128"), OP.add)

    def onward(t):
        zz, ls, lo = "zz%d" % t, "ls%d" % t, "lo%d" % t
        grp([(A("M", 0, 16), Z("Zw", s), A(zz, s, 256, 16)) for s in range(16)])
        cp(A("ui", 0, 16), A("M", 0, 16))
        ts(A("ui", 16, 32), A("ui", 0, 16), 4095, OP.bitwise_and)
        ts(A("ui", 32, 48), A("ui", 0, 16), 15, OP.bitwise_and)
        tt(A("uf", 0, 16), A("ui", 16, 32), A("ui", 16, 32), OP.mult)
        act(A("uf", 16, 32), A(ls, 16, 32), IDN, scale=592.0, bias=-1184.0 * 1024)
        tt(A("ui", 0, 16), A("uf", 0, 16), A("uf", 16, 32), OP.add)
        ts(A("ui", 48, 64), A("ui", 0, 16), 5, OP.arith_shift_right, 1023, OP.bitwise_and)
        if t < NV - 1:
            ts(A(lo, 16, 32), A("ui", 48, 64), 2.0, OP.mult)
            act(A(lo, 0, 16), A(ls, 16, 32), IDN, bias=-1.0)
            send(A("ls%d" % (t + 1)), A(lo))
            tt(LH1(t, 0), A("ui", 32, 48), A("Jn"), OP.add)
            ts(A("on"), LH1(t, 0), 2048.0, OP.add)
        else:
            LQ = lambda a: (T.lq[:, a, :], "lq", 16 * a, 16 * a + 16, 16)
            tt(LQ(0), A("ui", 32, 48), A("Jn"), OP.add)
            ts(LQ(1), A(ls, 0, 16), 0.5, OP.mult, -0.5, OP.add)
            ts(LQ(2), A(ls, 16, 32), 0.5, OP.mult, -1.0, OP.add)
            for h in range(2):
                ts(A("on", 8 * h, 8 * h + 8), (T.lq[:, 0, 8 * h:8 * h + 8], "lq", 0, 16, 8), 2048.0 * (1 - h), OP.add)
            cp(A("lv"), A("ui", 48, 64))
            grp([(A("M", 0, 256), A("Iq"), A("rw3", 256, 512))] + [(A("M", s, 256, 16), F("F3", s), A("lv")) for s in range(16)])
            act(A("OVP"), A("M", 0, 256), IDN)
            dma("Y", T.yvp[:], (T.OVP[0:128:16, :], "OVP", 0, 256, 256), 8192)

    def threshold(t):
        if t == 0:
            return -0.5
        grp([(A("M", 0, 1), A("onef"), A("acc", h, h + 1)) for h in range(2)])
        ts(A("ai", 0, 1), A("M", 0, 1), -0.5, OP.mult, 16384.0, OP.add)
        ts(A("ai", 1, 2), A("ai", 0, 1), 255, OP.bitwise_and)
        ts(A("thr"), A("ai", 1, 2), 16.0, OP.mult, -0.5, OP.add)
        return A("thr")

    def directories():
        for out, win, bias in (("OV", VDw, 2048.0), ("OPD", PDw, 2047.5)):
            for a in (0, 512):
                act(A("M"), win(a, a + 512), IDN, scale=0.5, bias=bias)
                tt(A(out, a, a + 512), win(a, a + 512), A("M"), OP.min)

    def packed(hh, qs):
        mm([(A("E%d" % hh), A(("Id", "Ia", "I4", "Ic")[q]), A("X", 1024 * q + 512 * hh, 1024 * q + 512 * hh + 512), q == 0, q == 3) for q in qs])

    for t in range(NV):
        last = t == NV - 1


        def do(name, fn, *args):
            at(t, name)
            return fn(*args)

        thr = do("thr", threshold, t)
        if t == 0:
            look1(0)
            for c in range(4):
                do("f%d" % c, look2, 0, L2_FIRST[c])
                if c:
                    do("l3%d" % (c - 1), look3, 0, c - 1)
            do("rows0", rows, 0)
            repeats(0, 0, 0, "ls0")
            do("ed0", edits, 0)
            do("on", onward, 0)
            do("g0", lines, 0, 0)
            do("l33", look3, 0, 3)
        else:
            do("l30", look3, t, 0)
            do("l31", look3, t, 1)
            for u in L2_LATER[AHEAD:]:
                do("l22", look2, t, u)
            do("l32", look3, t, 2)
            do("g0", lines, t, 0)
            do("l33", look3, t, 3)
            do("pd1", entries, t - 1, 1, 0)
            do("on", onward, t)
        do("e0", early, t, 0)
        do("g1", lines, t, 1)
        if last:
            do("dir", directories)
        do("t0", tail, t, 0, thr)
        do("n0", nearest, t, 0)
        do("g2", lines, t, 2)
        do("e1", early, t, 1)
        do("g3", lines, t, 3)
        do("x0", newline, t, 0)
        if last:
            packed(0, (0, 1))
            packed(1, (0, 1))
        else:
            do("ptr", pointers, t)
            do("l1", look1, t + 1)
            do("rows", rows, t + 1)
            do("l20", look2, t + 1, L2_LATER[0])
            for u in L2_LATER[1:AHEAD]:
                do("l21", look2, t + 1, u)
            do("ed", edits, t + 1)
        do("t1", tail, t, 1, thr)
        if last:
            dma("Y", T.yvd[:], A("OV", 0, 1024), 524288)
            dma("Y", T.ypd[:], A("OPD", 0, 1024), 1000000)
        do("n1", nearest, t, 1)
        do("x1", newline, t, 1)
        if last:
            dma("Y", T.yz[:], A("zn3"), 65536)
            for hh in range(2):
                packed(hh, (2, 3))
            act(A("OX", 0, 512), A("E0"), IDN)
            cp(A("OX", 512, 1024), A("E1"))
            dma("S", T.yx[:, 0:512], A("OX", 0, 512), 400000)
            dma("Y", T.yx[:, 512:1024], A("OX", 512, 1024), 600000)
    return ops


def depend(ops):
    deps = [set() for _ in ops]
    hist = {}
    for i, o in enumerate(ops):
        for lst, wr in ((o["r"], False), (o["w"], True)):
            for name, lo, hi in lst:
                for j, l2, h2, w2 in hist.get(name, ()):
                    if j != i and (((wr or w2) and lo < h2 and l2 < hi) or (name in PS and (ops[j]["e"] != o["e"] or o["e"] == "P"))):
                        deps[i].add(j)
        for lst, wr in ((o["r"], False), (o["w"], True)):
            for name, lo, hi in lst:
                h = hist.setdefault(name, [])
                if wr:
                    h[:] = [x for x in h if not (lo <= x[1] and x[2] <= hi and (name not in PS or ops[x[0]]["e"] == o["e"]))]
                h.append((i, lo, hi, wr))
    return deps


def key(o):
    nm = lambda a: (a[0][:2] if a[0][:2] in ("zn", "zz", "lo", "ls", "lh", "rw", "os", "GL", "GF") else a[0]) + str(a[1])
    return o["e"] + "".join(nm(a) for a in o["w"][:1] + o["r"][-1:])


def replay(ops, order, deps, C):
    free, fin, end = {e: 0.0 for e in ENG}, [0.0] * len(ops), 0.0
    for i in order:
        o = ops[i]
        e = o["e"]
        s = free[e]
        for j in deps[i]:
            d = ops[j]
            x = fin[j] + (d["x"][2] if d["k"] != "c" else C[5] if d["e"] != e else 0 if e == "P" else C[6])
            if x > s:
                s = x
        fin[i] = free[e] = s + o["d"]
        end = max(end, fin[i] + (o["x"][2] if o["k"] != "c" else 0))
    return end


def search(g, T, core, topo):
    vs = [build(g, T, core, topo, C) for C in COSTS]
    deps = depend(vs[0])
    ops, C = vs[0], COSTS[0]
    n = len(ops)
    gap = lambda j, i: ops[j]["x"][2] if ops[j]["k"] != "c" else C[5] if ops[j]["e"] != ops[i]["e"] else 0 if ops[j]["e"] == "P" else C[6]
    pre = [[(j, gap(j, i)) for j in deps[i]] for i in range(n)]
    post = [[] for _ in ops]
    for i in range(n):
        for j, d in pre[i]:
            post[j].append((i, d))
    tail = [o["x"][2] if o["k"] != "c" else 0.0 for o in ops]
    keys = [key(o) for o in ops]
    names = sorted(set(keys))

    def place(seq, edges, rel):
        st, busy = [0.0] * n, {e: [] for e in ENG}
        for i in seq:
            s, d, b = rel[i], ops[i]["d"], busy[ops[i]["e"]]
            for j, w in edges[i]:
                if st[j] + ops[j]["d"] + w > s:
                    s = st[j] + ops[j]["d"] + w
            k = len(b)
            while k > 0 and b[k - 1][1] > s:
                k -= 1
            while k < len(b) and b[k][0] < s + d:
                s = max(s, b[k][1])
                k += 1
            b.insert(k, (s, s + d))
            st[i] = s
        return st

    def topo_order(pr, edges, back):
        left, seq = [len(e) for e in edges], []
        heap = sorted((pr[i], i) for i in range(n) if left[i] == 0)
        while heap:
            i = heap.pop(0)[1]
            seq.append(i)
            new = False
            for j, w in back[i]:
                left[j] -= 1
                if left[j] == 0:
                    heap.append((pr[j], j))
                    new = True
            if new:
                heap.sort()
        return seq

    zero = [0.0] * n
    far = [0.0] * n
    for i in range(n - 1, -1, -1):
        far[i] = ops[i]["d"] + max([w + far[j] for j, w in post[i]] + [tail[i]])
    due = [o["at"] for o in ops]
    for i in range(n - 1, -1, -1):
        due[i] = min([due[i]] + [due[j] - w - ops[i]["d"] for j, w in post[i]])
    st = place(topo_order([due[i] - ops[i].get("b", 0.0) for i in range(n)], pre, post), pre, zero)
    if ROUNDS < 0:
        order = sorted(range(n), key=lambda i: (st[i], i))
        return order, [replay(o, order, deps, c) for o, c in zip(vs, COSTS)], st
    x, best, top = 12345, None, None
    for r in range(ROUNDS + 1):
        move = {}
        for m in range(r % 5 if r else 0):
            x = (x * 1103515245 + 12345) % 2147483648
            k = names[(x >> 8) % len(names)]
            x = (x * 1103515245 + 12345) % 2147483648
            move[k] = (-6, -3, -2, -1, 1, 2, 3, 6)[(x >> 8) % 8] * 400.0
        base = best[2] if best else st
        if r % 2 == 0:
            bk = place(topo_order([-base[i] - ops[i]["d"] - move.get(keys[i], 0.0) for i in range(n)], post, pre), post, tail)
            pr = [-bk[i] - ops[i]["d"] - ops[i].get("b", 0.0) for i in range(n)]
        else:
            pr = [base[i] + move.get(keys[i], 0.0) - ops[i].get("b", 0.0) for i in range(n)]
        fw = place(topo_order(pr, pre, post), pre, zero)
        order = sorted(range(n), key=lambda i: (fw[i], i))
        t = [replay(o, order, deps, c) for o, c in zip(vs, COSTS)]
        if best is None or sum(t) <= sum(best[0]) + SLACK * (1.0 - r / (0.8 * ROUNDS + 1)) * (x % 1000) / 1000.0 or sum(t) <= sum(best[0]):
            best = (t, order, fw)
        if top is None or sum(t) < sum(top[0]):
            top = best = (t, order, fw)
    return top[1], top[0], top[2]


def anneal(vs, deps, costs, order, rounds, heat, seed=12345):
    ops = vs[0]
    n = len(ops)
    reach, few = [], []
    for i in range(n):
        r = 0
        for j in deps[i]:
            r |= reach[j]
        few.append({j for j in deps[i] if not r >> j & 1 or ops[j]["k"] != "c"})
        for j in deps[i]:
            r |= 1 << j
        reach.append(r)
    deps = few
    lag = lambda o, C, j, i: o[j]["x"][2] if o[j]["k"] != "c" else C[5] if o[j]["e"] != o[i]["e"] else 0.0 if o[j]["e"] == "P" else C[6]
    pre = [[[(j, o[j]["d"] + lag(o, C, j, i)) for j in deps[i]] for i in range(n)] for o, C in zip(vs, costs)]
    dur = [[x["d"] for x in o] for o in vs]
    end = [[x["d"] + (x["x"][2] if x["k"] != "c" else 0.0) for x in o] for o in vs]
    post = [[] for _ in ops]
    for i in range(n):
        for j in deps[i]:
            post[j].append(i)
    need = [len(d) for d in deps]

    def run(seq):
        before, after = [-1] * n, [-1] * n
        left = list(need)
        for q in seq.values():
            for a, b in zip(q, q[1:]):
                before[b], after[a] = a, b
                left[b] += 1
        todo = [i for i in range(n) if left[i] == 0]
        for i in todo:
            for k in post[i]:
                left[k] -= 1
                if left[k] == 0:
                    todo.append(k)
            k = after[i]
            if k >= 0:
                left[k] -= 1
                if left[k] == 0:
                    todo.append(k)
        if len(todo) < n:
            return None
        sts, ts = [], []
        for p, d, e in zip(pre, dur, end):
            st = [0.0] * n
            for i in todo:
                k = before[i]
                s = st[k] + d[k] if k >= 0 else 0.0
                for j, w in p[i]:
                    w += st[j]
                    if w > s:
                        s = w
                st[i] = s
            sts.append(st)
            ts.append(max([a + b for a, b in zip(st, e)]))
        return ts, sts, before, todo

    def chain(res, m):
        ts, sts, before, todo = res
        st, out = sts[m], []
        i = max(range(n), key=lambda k: st[k] + end[m][k])
        while st[i] > 0:
            k = before[i]
            if k >= 0 and st[k] + dur[m][k] >= st[i] - 1e-6:
                if k not in deps[i] and ops[i]["e"] != "Y":
                    out.append((k, i))
                i = k
            else:
                i = max(pre[m][i], key=lambda x: st[x[0]] + x[1])[0]
        return out

    seq = {e: [i for i in order if ops[i]["e"] == e] for e in ENG}
    seq["Y"].sort()
    cur = run(seq)
    top, x = (cur, seq), seed
    chains = {}
    for r in range(rounds):
        x = (x * 1103515245 + 12345) % 2147483648
        m = (x >> 8) % len(vs)
        if m not in chains:
            chains[m] = chain(cur, m)
        if not chains[m]:
            continue
        x = (x * 1103515245 + 12345) % 2147483648
        a, b = chains[m][(x >> 8) % len(chains[m])]
        x = (x * 1103515245 + 12345) % 2147483648
        far, back = (0, 0, 1, 2, 4, 8, 16)[(x >> 8) % 7], (x >> 20) % 2
        e = ops[a]["e"]
        q = list(seq[e])
        p = q.index(a)
        if back:
            k = p
            while k > 0 and p - k < far and q[k - 1] not in deps[b]:
                k -= 1
            q.pop(p + 1)
            q.insert(k, b)
        else:
            k = p + 1
            while k + 1 < len(q) and k - p - 1 < far and a not in deps[q[k + 1]]:
                k += 1
            q.pop(p)
            q.insert(k, a)
        new = dict(seq)
        new[e] = q
        res = run(new)
        if res is None:
            continue
        x = (x * 1103515245 + 12345) % 2147483648
        if sum(res[0]) <= sum(cur[0]) + len(vs) * heat * (1.0 - r / rounds) * ((x >> 8) % 1000 / 1000.0) ** 2:
            cur, seq, chains = res, new, {}
            if sum(cur[0]) < sum(top[0][0]):
                top = (cur, seq)
    st = top[0][1][0]
    rank = {i: k for k, i in enumerate(top[0][3])}
    return sorted(range(n), key=lambda i: (st[i], rank[i])), top[0][0], st


def plan(g, T, core, topo):
    costs = [COSTS[k] for k in ANNEAL[0]]
    vs = [build(g, T, core, topo, C) for C in costs]
    return anneal(vs, depend(vs[0]), costs, search(g, T, core, topo)[0], ANNEAL[1], ANNEAL[2])


def emit(g, T, ops, order, deps):
    Q = {"V": g.vector, "S": g.scalar, "P": g.tensor, "G": g, "Y": g.sync}
    pos, cnt = {}, {e: 0 for e in ENG}
    clock = {e: {} for e in ENG}
    done, waits, need = {}, {}, set()
    for i in order:
        o = ops[i]
        e = o["e"]
        ck = clock[e]
        w = []
        for j in sorted(deps[i], key=lambda x: -pos[x][1]):
            d = ops[j]
            key, val = (d["e"], pos[j][0]) if d["k"] == "c" else (j, 1)
            if d["k"] == "c" and d["e"] == "P" and e == "P":
                continue
            if ck.get(key, 0) >= val:
                continue
            w.append(j)
            need.add(j)
            ck[key] = val
            if d["k"] != "rem":
                for k2, v2 in done[j].items():
                    if ck.get(k2, 0) < v2:
                        ck[k2] = v2
        waits[i] = w
        cnt[e] += 1
        pos[i] = (cnt[e], len(pos))
        done[i] = dict(ck)
    num, tot, sent, dmas = {}, {e: 0 for e in ENG}, 0, []
    for i in order:
        o = ops[i]
        q = Q[o["e"]]
        for j in waits[i]:
            d = ops[j]
            if d["k"] == "c":
                q.wait_ge(T.sem["e" + d["e"]], num[j])
            else:
                q.wait_ge(d["x"][0], d["x"][1])
        r = o["fn"]()
        if o["k"] == "c":
            if i in need:
                tot[o["e"]] += 1
                num[i] = tot[o["e"]]
                r.then_inc(T.sem["e" + o["e"]], 1)
        else:
            if i not in need:
                dmas.append(o)
            if o["k"] == "rem":
                sent += o["x"][1]
    g.wait_ge(T.sem.sent, sent)
    for o in dmas:
        Q[o["e"]].wait_ge(o["x"][0], o["x"][1])


def rank_program(g, core, T, topo):
    if T.rank_of(core) is None:
        return
    if not PLAN:
        PLAN.append(plan(g, T, core, topo)[0])
    ops = build(g, T, core, topo, COSTS[0])
    emit(g, T, ops, PLAN[0], depend(ops))
